import numpy as np
import ml_dtypes


def mxq(x, axis, fmt="e4m3"):
    dtype, down = {"e4m3": (ml_dtypes.float8_e4m3fn, 7), "e5m2": (ml_dtypes.float8_e5m2, 14)}[fmt]
    v = np.moveaxis(np.asarray(x, np.float32).astype(ml_dtypes.bfloat16).astype(np.float64), axis, -1)
    blocks = v.reshape(v.shape[:-1] + (-1, 32))
    amax = np.abs(blocks).max(-1, keepdims=True)
    byte = np.maximum(np.where(amax > 0, np.frexp(amax)[1] - 1 + 127, 0) - down, 1)
    scale = np.exp2(byte - 127.0)
    codes = (blocks / scale).astype(np.float32).astype(dtype).astype(np.float64)
    return np.moveaxis((codes * scale).reshape(v.shape), -1, axis)


WIDE = False


def mx_kscale(k):
    if not WIDE:
        return np.ones(k)
    levels = np.array([10, -10, 5, -5, 0])
    if k % 512:
        return np.exp2(np.random.permutation(np.resize(levels, k // 32))).repeat(32)
    a = np.empty((k // 512, 16))
    for p in range(k // 512):
        a[p, :8] = np.random.permutation(np.resize(levels, 8))
        for g in range(8):
            far = levels[np.abs(levels - a[p, g]) >= 10]
            a[p, g + 8] = far[np.random.randint(len(far))]
    return np.exp2(a.ravel()).repeat(32)


def f64(x):
    return np.asarray(x).astype(np.float64)


def striped(idx):
    return np.tile(idx.reshape(-1, 16).T, (8, 1)).astype(np.uint16)


def unstriped(offs):
    return offs[:16].T.reshape(-1).astype(np.int64)


E2M1 = np.array([0.0, 0.5, 1.0, 1.5, 2.0, 3.0, 4.0, 6.0, -0.0, -0.5, -1.0, -1.5, -2.0, -3.0, -4.0, -6.0])


def pack_weight(w, fmt):
    k, n = w.shape
    w = f64(np.asarray(w, np.float32).astype(ml_dtypes.bfloat16)).reshape(k // 32, 32, n)
    amax = np.abs(w).max(1)
    if fmt == "e4m3":
        byte = np.frexp(amax)[1] - 1 + 127 - 7
    else:
        mant, ex = np.frexp(amax / 6.0)
        byte = np.where(mant > 0.5, ex, ex - 1) + 127
    byte = np.clip(np.where(amax > 0, byte, 1), 1, 254)
    scaled = (w * np.exp2(127.0 - byte)[:, None, :]).reshape(k, n).astype(np.float32)
    by_word = np.ascontiguousarray(scaled.reshape(k // 512, 128, 4, n).transpose(0, 1, 3, 2))
    if fmt == "e4m3":
        words = by_word.astype(ml_dtypes.float8_e4m3fn).view(np.uint8)
    else:
        c = by_word.astype(ml_dtypes.float4_e2m1fn).view(np.uint8) & 0xF
        words = (c[..., 0::2] | (c[..., 1::2] << 4)).reshape(k // 512, 128, 2 * n)
    return np.ascontiguousarray(words), np.ascontiguousarray(byte.astype(np.uint8).reshape(k // 512, 16, n))


def unpack_weight(words, scales, fmt):
    g, _, n = scales.shape
    words = np.ascontiguousarray(words).reshape(g, 128, n, -1)
    if fmt == "e4m3":
        vals = words.view(ml_dtypes.float8_e4m3fn).astype(np.float64)
    else:
        nib = np.empty((g, 128, n, 4), np.uint8)
        nib[..., 0::2] = words & 0xF
        nib[..., 1::2] = words >> 4
        vals = E2M1[nib]
    vals = vals * np.repeat(np.exp2(scales.astype(np.float64) - 127.0), 8, axis=1)[..., None]
    return vals.transpose(0, 1, 3, 2).reshape(g * 512, n)


def gelu(v):
    return 0.5 * v * (1.0 + np.tanh(np.sqrt(2.0 / np.pi) * (v + 0.044715 * v**3)))


K, T, S, P, H, N = 1536, 4096, 1024, 512, 1024, 768

def setup_inputs():
    n = np.random.standard_normal
    s = mx_kscale(K)[:, None]
    u = mx_kscale(H)[:, None]
    tab_words, tab_scales = pack_weight(n((K, T)) * s, "e4m3")
    wox_words, wox_scales = pack_weight(n((H, N)) / np.sqrt(H) / u, "e2m1")
    return {
        "tab_words": tab_words, "tab_scales": tab_scales,
        "offs": striped(np.random.permutation(T)[:S]),
        "pos1": striped(np.random.permutation(S)[:P]),
        "pos2": striped(np.random.permutation(S)[:P]),
        "pos3": striped(np.random.permutation(S)[:P]),
        "w1": (n((K, H)) / np.sqrt(K) / s).astype(np.float32),
        "gain": (np.random.uniform(0.75, 2.0, H) * u[:, 0]).astype(np.float32),
        "wox_words": wox_words, "wox_scales": wox_scales,
        "wrd": (n((H, N)) / np.sqrt(H) / u).astype(np.float32),
    }

def reference(tab_words, tab_scales, offs, pos1, pos2, pos3, w1, gain, wox_words, wox_scales, wrd):
    v = unpack_weight(tab_words, tab_scales, "e4m3")[:, unstriped(offs)]
    h = mxq(f64(w1), 0, "e4m3").T @ v
    rim = h[:, unstriped(pos1)]
    body = h[:, unstriped(pos2)]
    base = h[:, unstriped(pos3)]
    quot = body * base / (1.0 + np.square(rim))
    z = mxq(quot * f64(gain)[:, None], 0, "e4m3")
    yox = unpack_weight(wox_words, wox_scales, "e2m1").T @ z
    yrd = mxq(f64(wrd), 0, "e4m3").T @ z
    return np.maximum(yox, yrd)

@@ -1,0 +1,345 @@
+from contextlib import ExitStack
+
+import concourse.mybir as mybir
+
+K, T, S, M, H, N = 1536, 4096, 1024, 512, 1024, 768
+FLOPS = 2 * K * H * S + 2 * 2 * H * N * M
+
+F32 = mybir.dt.float32
+BF16 = mybir.dt.bfloat16
+I32 = mybir.dt.int32
+U32 = mybir.dt.uint32
+U16 = mybir.dt.uint16
+U8 = mybir.dt.uint8
+FP8X4 = mybir.dt.float8_e4m3fn_x4
+FP4X4 = mybir.dt.float4_e2m1fn_x4
+ACT = mybir.ActivationFunctionType
+MULT = mybir.AluOpType.mult
+MAX = mybir.AluOpType.max
+
+P = 128
+PACK = 4
+KP = P * PACK
+BANK = 512
+
+
+def tile_list_sherd_vessel_joining_kernel(
+    tc, tab_words, tab_scales, offs, pos1, pos2, pos3, w1, gain, wox_words, wox_scales, wrd, out
+):
+    nc = tc.nc
+    ka = K // KP
+    hb = H // KP
+    with ExitStack() as ctx:
+        keep = ctx.enter_context(tc.tile_pool(name="keep", bufs=1))
+        ring = ctx.enter_context(tc.tile_pool(name="ring", bufs=2))
+        psum = ctx.enter_context(tc.psum_pool(name="psum", bufs=8))
+
+        offs_t = keep.tile([P, S // 16], U16, name="offs_t")
+        nc.sync.dma_start(offs_t[:], offs)
+
+        tab_sc = keep.tile([P, T], U8, name="tab_sc", align_bytes=64)
+        wox_sc = keep.tile([P, hb, N], U8, name="wox_sc", align_bytes=64)
+        warm = keep.tile([P, 2], F32, name="warm")
+        nc.vector.memset(tab_sc[:].bitcast(I32), 0)
+        nc.vector.memset(wox_sc[:].rearrange("p a n -> p (a n)").bitcast(I32), 0)
+        nc.vector.memset(warm[:, 0:1], 1.0)
+        nc.scalar.activation(warm[:, 1:2], warm[:, 0:1], ACT.Abs_reciprocal_sqrt)
+
+        tab_w = []
+        for a in range(ka):
+            tw = keep.tile([P, T], U32, name="tab_w%d" % a, align_bytes=64)
+            nc.sync.dma_start(tw[:].bitcast(I32), tab_words[a].rearrange("p t i -> p (t i)").bitcast(I32))
+            tab_w.append(tw)
+            if a == 0:
+                for q in range(4):
+                    nc.sync.dma_start(
+                        tab_sc[32 * q : 32 * q + 4 * ka, :].bitcast(I32),
+                        tab_scales[:, 4 * q : 4 * q + 4, :].bitcast(I32),
+                    )
+        gain_t = keep.tile([P, hb, PACK], F32, name="gain_t")
+        nc.gpsimd.dma_start(gain_t[:], gain.rearrange("(b p t) -> p b t", b=hb, t=PACK))
+        gain_row = []
+        for b, w in enumerate((M, M // 2)):
+            gr = keep.tile([P, PACK, w], F32, name="gain_row%d" % b, align_bytes=64)
+            nc.scalar.copy(gr[:], gain_t[:, b, :].unsqueeze(2).to_broadcast([P, PACK, w]))
+            gain_row.append(gr)
+        for q in range(4):
+            nc.gpsimd.dma_start(
+                wox_sc[32 * q : 32 * q + 4, :, :].bitcast(I32),
+                wox_scales[:, 4 * q : 4 * q + 4, :].rearrange("a r n -> r a n").bitcast(I32),
+            )
+
+        def load_rows(src, r0, c0, width):
+            raw = ring.tile([P, PACK, width], F32, name="raw", tag="raw", bufs=4, align_bytes=64)
+            nc.sync.dma_start(raw[:], src[r0 : r0 + KP, c0 : c0 + width].rearrange("(p j) c -> p j c", j=PACK))
+            return raw
+
+        w1_raw = {}
+        for a in range(ka):
+            w1_raw[(0, a)] = load_rows(w1, a * KP, 0, KP)
+        pos_t = []
+        for i, pos in enumerate((pos1, pos2, pos3)):
+            pt = keep.tile([P, M // 16], U16, name="pos_t%d" % i)
+            nc.sync.dma_start(pt[:], pos)
+            pos_t.append(pt)
+        for a in range(ka):
+            w1_raw[(1, a)] = load_rows(w1, a * KP, KP, KP)
+        wox_w = keep.tile([P, hb, 2 * N], U8, name="wox_w", align_bytes=64)
+        nc.sync.dma_start(wox_w[:].bitcast(I32), wox_words.rearrange("a p c -> p a c").bitcast(I32))
+        wrd_parts = [(b, c0, wd) for b in range(hb) for c0, wd in ((0, 512), (512, 256))]
+        wrd_raw = {}
+        for b, c0, wd in wrd_parts:
+            wrd_raw[(b, c0)] = load_rows(wrd, b * KP, c0, wd)
+
+        v_w = []
+        v_sc = keep.tile([P, S], U8, name="v_sc", align_bytes=64)
+        for a in range(ka):
+            vw = keep.tile([P, S], U32, name="v_w%d" % a, align_bytes=64)
+            nc.vector.tensor_copy(vw[:], tab_w[a][:].indirect(offs_t[:]))
+            v_w.append(vw)
+            if a == 0:
+                nc.vector.tensor_copy(v_sc[:], tab_sc[:].indirect(offs_t[:]))
+
+        def grouped(width):
+            return ring.tile([P, PACK * width], BF16, name="grp", tag="grp", bufs=3, align_bytes=64)
+
+        def copy_on(engine, dst, src):
+            if engine == "v":
+                nc.vector.tensor_copy(dst, src)
+            else:
+                nc.scalar.copy(dst, src)
+
+        w1_grp, w1_q = {}, {}
+
+        def cast_w1(b, a, u, engine):
+            g = ring.tile([P, 2 * P * PACK], BF16, name="grph", tag="grph", bufs=4, align_bytes=64)
+            src = w1_raw[(b, a)][:].rearrange("p j (m t) -> p m j t", t=PACK)
+            copy_on(engine, g[:].rearrange("p (t m j) -> p m j t", t=2, j=PACK), src[:, :, :, 2 * u : 2 * u + 2])
+            w1_grp[(b, a, u)] = g
+
+        def quantize(name, grp, width):
+            codes = keep.tile([P, width], U32, name=name + "_c", align_bytes=64)
+            scales = keep.tile([P, width], U8, name=name + "_s", align_bytes=64)
+            nc.vector.quantize_mx(out=codes[:].bitcast(FP8X4), scales=scales[:], in_=grp[:])
+            return codes, scales
+
+        def quant_w1(b, a, u):
+            w1_q[(b, a, u)] = quantize("w1q%d%d%d" % (b, a, u), w1_grp[(b, a, u)], 2 * P)
+
+        h_ps, h_sb = {}, {}
+
+        def h_pass(b, t, half, a):
+            if a == 0:
+                h_ps[(b, t, half)] = psum.tile([P, BANK], F32, name="bank", tag="bank")
+            codes, scales = w1_q[(b, a, t // 2)]
+            cols = slice(half * BANK, (half + 1) * BANK)
+            nc.tensor.matmul_mx(
+                out=h_ps[(b, t, half)][:],
+                lhsT=codes[:, (t % 2) * P : (t % 2 + 1) * P].bitcast(FP8X4),
+                lhsT_scale=scales[:, (t % 2) * P : (t % 2 + 1) * P],
+                rhs=v_w[a][:, cols].bitcast(FP8X4),
+                rhs_scale=v_sc[4 * a : P, cols],
+                start=(a == 0),
+                stop=(a == ka - 1),
+            )
+
+        def h_out(b, t, half, engine):
+            if half == 0:
+                h_sb[(b, t)] = ring.tile([P, S], F32, name="h", tag="h", bufs=5, align_bytes=64)
+            copy_on(engine, h_sb[(b, t)][:, half * BANK : (half + 1) * BANK], h_ps[(b, t, half)][:])
+
+        def h_tile_out(b, t):
+            h_out(b, t, 0, "s")
+            h_out(b, t, 1, "s")
+
+        damp, quot, z_q = {}, {}, {}
+
+        def picked(b, t, which, m0, w):
+            return h_sb[(b, t)][:].indirect(pos_t[which][:, m0 // 16 : (m0 + w) // 16])
+
+        body = {}
+
+        def rim(b, t, m0, w):
+            if t == 0:
+                damp[(b, m0)] = keep.tile([P, PACK, w], F32, name="damp%d_%d" % (b, m0), align_bytes=64)
+            nc.vector.tensor_copy(damp[(b, m0)][:, t, :], picked(b, t, 0, m0, w))
+
+        def damping(b, m0, w, t0, t1):
+            x = damp[(b, m0)][:, t0:t1, :]
+            nc.scalar.activation(x, x, ACT.Square)
+            nc.scalar.activation(x, x, ACT.Abs_reciprocal_sqrt, bias=1.0)
+            nc.scalar.activation(x, x, ACT.Square)
+
+        def pick_body(b, t, m0, w):
+            bd = ring.tile([P, w], F32, name="body", tag="body", align_bytes=64)
+            nc.vector.tensor_tensor(bd[:], picked(b, t, 1, m0, w), gain_row[b][:, t, :], MULT)
+            body[(b, t, m0)] = bd
+
+        def pick_base(b, t, m0, w):
+            if t == 0:
+                quot[(b, m0)] = keep.tile([P, PACK, w], F32, name="quot%d_%d" % (b, m0), align_bytes=64)
+            nc.vector.tensor_tensor(quot[(b, m0)][:, t, :], picked(b, t, 2, m0, w), body[(b, t, m0)][:], MULT)
+
+        z_grp = {}
+
+        def z_round(b, m0, w):
+            zg = grouped(w)
+            nc.vector.tensor_tensor(
+                zg[:].rearrange("p (c i t) -> p c t i", i=4, t=PACK),
+                quot[(b, m0)][:].rearrange("p t (c i) -> p c t i", i=4),
+                damp[(b, m0)][:].rearrange("p t (c i) -> p c t i", i=4),
+                MULT,
+            )
+            z_grp[(b, m0)] = zg
+
+        def z_quant(b, m0, w):
+            z_q[(b, m0)] = quantize("zq%d_%d" % (b, m0), z_grp[(b, m0)], w)
+
+        wrd_grp, wrd_q = {}, {}
+
+        def cast_wrd(b, c0, wd, engine):
+            g = grouped(wd)
+            copy_on(
+                engine,
+                g[:].rearrange("p (c i j) -> p c j i", i=4, j=PACK),
+                wrd_raw[(b, c0)][:].rearrange("p j (c i) -> p c j i", i=4),
+            )
+            wrd_grp[(b, c0)] = g
+
+        def quant_wrd(b, c0, wd):
+            wrd_q[(b, c0)] = quantize("wrdq%d_%d" % (b, c0), wrd_grp[(b, c0)], wd)
+
+        y_ps = {}
+
+        def y_pass(b, m0, w, pair):
+            zc, zs = z_q[(0, 0)] if b == 0 else z_q[(1, m0)]
+            z0 = m0 if b == 0 else 0
+            if b == 0:
+                y_ps[(m0, pair, 0)] = psum.tile([P, BANK], F32, name="bank", tag="bank")
+                y_ps[(m0, pair, 1)] = psum.tile([P, BANK], F32, name="bank", tag="bank")
+            for u in range(2):
+                n0 = (2 * pair + u) * P
+                for s in range(w // P):
+                    nc.tensor.matmul_mx(
+                        out=y_ps[(m0, pair, 0)][:, u * w + s * P : u * w + (s + 1) * P],
+                        lhsT=wox_w[:, b, 2 * n0 : 2 * (n0 + P)].bitcast(FP4X4),
+                        lhsT_scale=wox_sc[:, b, n0 : n0 + P],
+                        rhs=zc[:, z0 + s * P : z0 + (s + 1) * P].bitcast(FP8X4),
+                        rhs_scale=zs[:, z0 + s * P : z0 + (s + 1) * P],
+                        start=(b == 0 and u == 0 and s == 0),
+                        stop=(b == hb - 1 and u == 1 and s == w // P - 1),
+                    )
+            for u in range(2):
+                n0 = (2 * pair + u) * P
+                c0 = 0 if n0 < 512 else 512
+                wc, ws = wrd_q[(b, c0)]
+                nc.tensor.matmul_mx(
+                    out=y_ps[(m0, pair, 1)][:, u * w : (u + 1) * w],
+                    lhsT=wc[:, n0 - c0 : n0 - c0 + P].bitcast(FP8X4),
+                    lhsT_scale=ws[:, n0 - c0 : n0 - c0 + P],
+                    rhs=zc[:, z0 : z0 + w].bitcast(FP8X4),
+                    rhs_scale=zs[:, z0 : z0 + w],
+                    start=(b == 0 and u == 0),
+                    stop=(b == hb - 1 and u == 1),
+                )
+
+        def y_out(m0, w, pair):
+            ox = ring.tile([P, 2 * w], F32, name="ox", tag="ox", align_bytes=64)
+            nc.scalar.copy(ox[:], y_ps[(m0, pair, 0)][:, 0 : 2 * w])
+            res = ring.tile([P, 2 * w], F32, name="res", tag="res", bufs=4, align_bytes=64)
+            nc.vector.tensor_tensor(res[:], y_ps[(m0, pair, 1)][:, 0 : 2 * w], ox[:], MAX)
+            nc.sync.dma_start(
+                out[2 * pair * P : (2 * pair + 2) * P, m0 : m0 + w].rearrange("(u p) m -> p u m", u=2),
+                res[:].rearrange("p (u m) -> p u m", u=2),
+            )
+
+        for a in range(ka):
+            cast_w1(0, a, 0, "v")
+            cast_w1(0, a, 1, "s")
+            quant_w1(0, a, 0)
+            for t in range(2):
+                for half in range(2):
+                    h_pass(0, t, half, a)
+            quant_w1(0, a, 1)
+            if a == ka - 1:
+                h_out(0, 0, 0, "s")
+                h_out(0, 0, 1, "v")
+            for t in range(2, PACK):
+                for half in range(2):
+                    h_pass(0, t, half, a)
+        for t in range(1, PACK):
+            h_tile_out(0, t)
+        for u in range(2):
+            for a in range(ka):
+                cast_w1(1, a, u, "s")
+
+        def h_tile(b, t):
+            for half in range(2):
+                for a in range(ka):
+                    h_pass(b, t, half, a)
+
+        def picks(b, t, m0, w):
+            pick_body(b, t, m0, w)
+            rim(b, t, m0, w)
+            pick_base(b, t, m0, w)
+
+        W = 256
+        picks(0, 0, 0, M)
+        picks(0, 1, 0, M)
+        for a in range(ka):
+            quant_w1(1, a, 0)
+        h_tile(1, 0)
+        h_tile(1, 1)
+        h_tile_out(1, 0)
+        h_tile_out(1, 1)
+        picks(0, 2, 0, M)
+        for a in range(ka):
+            quant_w1(1, a, 1)
+        h_tile(1, 2)
+        h_tile(1, 3)
+        damping(0, 0, M, 0, 2)
+        h_tile_out(1, 2)
+        h_tile_out(1, 3)
+        picks(0, 3, 0, M)
+        damping(0, 0, M, 2, 4)
+        cast_wrd(0, 0, 512, "s")
+        cast_wrd(0, 512, 256, "s")
+        for t in range(PACK):
+            picks(1, t, 0, W)
+        damping(1, 0, W, 0, 4)
+        z_round(0, 0, M)
+        for t in range(PACK):
+            rim(1, t, W, W)
+        z_quant(0, 0, M)
+        cast_wrd(1, 0, 512, "s")
+        cast_wrd(1, 512, 256, "s")
+        damping(1, W, W, 0, 4)
+        quant_wrd(0, 0, 512)
+        quant_wrd(0, 512, 256)
+        for pair in range(3):
+            y_pass(0, 0, W, pair)
+        pick_body(1, 0, W, W)
+        pick_body(1, 1, W, W)
+        pick_base(1, 0, W, W)
+        z_round(1, 0, W)
+        pick_base(1, 1, W, W)
+        z_quant(1, 0, W)
+        pick_body(1, 2, W, W)
+        pick_body(1, 3, W, W)
+        quant_wrd(1, 0, 512)
+        quant_wrd(1, 512, 256)
+        for pair in range(3):
+            y_pass(1, 0, W, pair)
+        pick_base(1, 2, W, W)
+        pick_base(1, 3, W, W)
+        y_out(0, W, 0)
+        z_round(1, W, W)
+        y_pass(0, W, W, 0)
+        y_out(0, W, 1)
+        z_quant(1, W, W)
+        y_pass(0, W, W, 1)
+        y_out(0, W, 2)
+        y_pass(0, W, W, 2)
+        for pair in range(3):
+            y_pass(1, W, W, pair)
+            y_out(W, W, pair)

@@ -19,327 +19,333 @@ MAX = mybir.AluOpType.max
 
 P = 128
 PACK = 4
-KP = P * PACK
+PASS = P * PACK
+K_PASSES = K // PASS
+R_PASSES = H // PASS
+QUADRANTS = 4
+LIST_GROUP = 16
 BANK = 512
+LINE = 4
+M_HALF = M // 2
+PAIRS = N // (2 * P)
+WRD_PARTS = ((0, 512), (512, 256))
+RIM, BODY, BASE = 0, 1, 2
+OX, RD = 0, 1
+LAST = PACK - 1
 
 
 def tile_list_sherd_vessel_joining_kernel(
     tc, tab_words, tab_scales, offs, pos1, pos2, pos3, w1, gain, wox_words, wox_scales, wrd, out
 ):
     nc = tc.nc
-    ka = K // KP
-    hb = H // KP
     with ExitStack() as ctx:
         keep = ctx.enter_context(tc.tile_pool(name="keep", bufs=1))
         ring = ctx.enter_context(tc.tile_pool(name="ring", bufs=2))
         psum = ctx.enter_context(tc.psum_pool(name="psum", bufs=8))
 
-        offs_t = keep.tile([P, S // 16], U16, name="offs_t")
-        nc.sync.dma_start(offs_t[:], offs)
+        def kept(shape, dtype, name):
+            return keep.tile(shape, dtype, name=name, align_bytes=64)
 
-        tab_sc = keep.tile([P, T], U8, name="tab_sc", align_bytes=64)
-        wox_sc = keep.tile([P, hb, N], U8, name="wox_sc", align_bytes=64)
-        warm = keep.tile([P, 2], F32, name="warm")
-        nc.vector.memset(tab_sc[:].bitcast(I32), 0)
-        nc.vector.memset(wox_sc[:].rearrange("p a n -> p (a n)").bitcast(I32), 0)
-        nc.vector.memset(warm[:, 0:1], 1.0)
-        nc.scalar.activation(warm[:, 1:2], warm[:, 0:1], ACT.Abs_reciprocal_sqrt)
+        def reused(shape, dtype, tag, bufs):
+            return ring.tile(shape, dtype, name=tag, tag=tag, bufs=bufs, align_bytes=64)
 
-        tab_w = []
-        for a in range(ka):
-            tw = keep.tile([P, T], U32, name="tab_w%d" % a, align_bytes=64)
-            nc.sync.dma_start(tw[:].bitcast(I32), tab_words[a].rearrange("p t i -> p (t i)").bitcast(I32))
-            tab_w.append(tw)
-            if a == 0:
-                for q in range(4):
-                    nc.sync.dma_start(
-                        tab_sc[32 * q : 32 * q + 4 * ka, :].bitcast(I32),
-                        tab_scales[:, 4 * q : 4 * q + 4, :].bitcast(I32),
-                    )
-        gain_t = keep.tile([P, hb, PACK], F32, name="gain_t")
-        nc.gpsimd.dma_start(gain_t[:], gain.rearrange("(b p t) -> p b t", b=hb, t=PACK))
-        gain_row = []
-        for b, w in enumerate((M, M // 2)):
-            gr = keep.tile([P, PACK, w], F32, name="gain_row%d" % b, align_bytes=64)
-            nc.scalar.copy(gr[:], gain_t[:, b, :].unsqueeze(2).to_broadcast([P, PACK, w]))
-            gain_row.append(gr)
-        for q in range(4):
-            nc.gpsimd.dma_start(
-                wox_sc[32 * q : 32 * q + 4, :, :].bitcast(I32),
-                wox_scales[:, 4 * q : 4 * q + 4, :].rearrange("a r n -> r a n").bitcast(I32),
-            )
-
-        def load_rows(src, r0, c0, width):
-            raw = ring.tile([P, PACK, width], F32, name="raw", tag="raw", bufs=4, align_bytes=64)
-            nc.sync.dma_start(raw[:], src[r0 : r0 + KP, c0 : c0 + width].rearrange("(p j) c -> p j c", j=PACK))
+        def load_rows(src, row0, col0, width):
+            raw = reused([P, PACK, width], F32, "raw", 4)
+            rows = src[row0 : row0 + PASS, col0 : col0 + width]
+            nc.sync.dma_start(raw[:], rows.rearrange("(p j) c -> p j c", j=PACK))
             return raw
 
-        w1_raw = {}
-        for a in range(ka):
-            w1_raw[(0, a)] = load_rows(w1, a * KP, 0, KP)
+        offs_t = keep.tile([P, S // LIST_GROUP], U16, name="offs_t")
+        nc.sync.dma_start(offs_t[:], offs)
+
+        tab_sc = kept([P, T], U8, "tab_sc")
+        wox_sc = kept([P, R_PASSES, N], U8, "wox_sc")
+        nc.vector.memset(tab_sc[:].bitcast(I32), 0)
+        nc.vector.memset(wox_sc[:].rearrange("p b n -> p (b n)").bitcast(I32), 0)
+
+        w1_raw, tab_w = {}, []
+        for a in range(K_PASSES):
+            words = kept([P, T], U32, "tab_w%d" % a)
+            nc.sync.dma_start(words[:].bitcast(I32), tab_words[a].rearrange("p t i -> p (t i)").bitcast(I32))
+            tab_w.append(words)
+            if a == 0:
+                for q in range(QUADRANTS):
+                    nc.sync.dma_start(
+                        tab_sc[32 * q : 32 * q + 4 * K_PASSES, :].bitcast(I32),
+                        tab_scales[:, 4 * q : 4 * q + 4, :].bitcast(I32),
+                    )
+            w1_raw[(0, a)] = load_rows(w1, a * PASS, 0, PASS)
+
+        gain_t = keep.tile([P, R_PASSES, PACK], F32, name="gain_t")
+        nc.gpsimd.dma_start(gain_t[:], gain.rearrange("(b p t) -> p b t", b=R_PASSES, t=PACK))
+        gain_rows = []
+        for b in range(R_PASSES):
+            rows = reused([P, PACK, M], F32, "gain_rows%d" % b, 1)
+            nc.scalar.activation(rows[:], gain_t[:, b, :].unsqueeze(2).to_broadcast([P, PACK, M]), ACT.Copy)
+            gain_rows.append(rows)
+        for q in range(QUADRANTS):
+            nc.gpsimd.dma_start(
+                wox_sc[32 * q : 32 * q + 4, :, :].bitcast(I32),
+                wox_scales[:, 4 * q : 4 * q + 4, :].rearrange("b r n -> r b n").bitcast(I32),
+            )
+
         pos_t = []
-        for i, pos in enumerate((pos1, pos2, pos3)):
-            pt = keep.tile([P, M // 16], U16, name="pos_t%d" % i)
-            nc.sync.dma_start(pt[:], pos)
-            pos_t.append(pt)
-        for a in range(ka):
-            w1_raw[(1, a)] = load_rows(w1, a * KP, KP, KP)
-        wox_w = keep.tile([P, hb, 2 * N], U8, name="wox_w", align_bytes=64)
-        nc.sync.dma_start(wox_w[:].bitcast(I32), wox_words.rearrange("a p c -> p a c").bitcast(I32))
-        wrd_parts = [(b, c0, wd) for b in range(hb) for c0, wd in ((0, 512), (512, 256))]
+        for which, pos in enumerate((pos1, pos2, pos3)):
+            entries = keep.tile([P, M // LIST_GROUP], U16, name="pos_t%d" % which)
+            nc.sync.dma_start(entries[:], pos)
+            pos_t.append(entries)
+        for a in range(K_PASSES):
+            w1_raw[(1, a)] = load_rows(w1, a * PASS, PASS, PASS)
+        wox_w = kept([P, R_PASSES, 2 * N], U8, "wox_w")
+        nc.sync.dma_start(wox_w[:].bitcast(I32), wox_words.rearrange("b p c -> p b c").bitcast(I32))
         wrd_raw = {}
-        for b, c0, wd in wrd_parts:
-            wrd_raw[(b, c0)] = load_rows(wrd, b * KP, c0, wd)
+        for b in range(R_PASSES):
+            for part, (col0, width) in enumerate(WRD_PARTS):
+                wrd_raw[(b, part)] = load_rows(wrd, b * PASS, col0, width)
 
         v_w = []
-        v_sc = keep.tile([P, S], U8, name="v_sc", align_bytes=64)
-        for a in range(ka):
-            vw = keep.tile([P, S], U32, name="v_w%d" % a, align_bytes=64)
-            nc.vector.tensor_copy(vw[:], tab_w[a][:].indirect(offs_t[:]))
-            v_w.append(vw)
+        v_sc = kept([P, S], U8, "v_sc")
+        for a in range(K_PASSES):
+            words = kept([P, S], U32, "v_w%d" % a)
+            nc.vector.tensor_copy(words[:], tab_w[a][:].indirect(offs_t[:]))
+            v_w.append(words)
             if a == 0:
                 nc.vector.tensor_copy(v_sc[:], tab_sc[:].indirect(offs_t[:]))
 
-        def grouped(width):
-            return ring.tile([P, PACK * width], BF16, name="grp", tag="grp", bufs=3, align_bytes=64)
-
-        def copy_on(engine, dst, src):
-            if engine == "v":
-                nc.vector.tensor_copy(dst, src)
-            else:
-                nc.scalar.copy(dst, src)
-
-        w1_grp, w1_q = {}, {}
-
-        def cast_w1(b, a, u, engine):
-            g = ring.tile([P, 2 * P * PACK], BF16, name="grph", tag="grph", bufs=4, align_bytes=64)
-            src = w1_raw[(b, a)][:].rearrange("p j (m t) -> p m j t", t=PACK)
-            copy_on(engine, g[:].rearrange("p (t m j) -> p m j t", t=2, j=PACK), src[:, :, :, 2 * u : 2 * u + 2])
-            w1_grp[(b, a, u)] = g
-
-        def quantize(name, grp, width):
-            codes = keep.tile([P, width], U32, name=name + "_c", align_bytes=64)
-            scales = keep.tile([P, width], U8, name=name + "_s", align_bytes=64)
-            nc.vector.quantize_mx(out=codes[:].bitcast(FP8X4), scales=scales[:], in_=grp[:])
+        def quantize(name, rounded, width):
+            codes = kept([P, width], U32, name + "_codes")
+            scales = kept([P, width], U8, name + "_scales")
+            nc.vector.quantize_mx(out=codes[:].bitcast(FP8X4), scales=scales[:], in_=rounded[:])
             return codes, scales
 
-        def quant_w1(b, a, u):
-            w1_q[(b, a, u)] = quantize("w1q%d%d%d" % (b, a, u), w1_grp[(b, a, u)], 2 * P)
+        def turn(shape, dtype, u):
+            return reused(shape, dtype, "turn%d" % u, 1)
+
+        def narrow():
+            return reused([P, 2 * P * PACK], BF16, "narrow", 4)
+
+        w1_rounded, w1_q = {}, {}
+
+        def round_w1(b, a, u, copy):
+            rounded = turn([P, 2 * P * PACK], BF16, u) if (b, a) == (1, K_PASSES - 1) else narrow()
+            src = w1_raw[(b, a)][:].rearrange("p j (m t) -> p m j t", t=PACK)
+            copy(rounded[:].rearrange("p (s m j) -> p m j s", s=2, j=PACK), src[:, :, :, 2 * u : 2 * u + 2])
+            w1_rounded[(b, a, u)] = rounded
+
+        def quantize_w1(b, a, u):
+            w1_q[(b, a, u)] = quantize("w1_%d%d%d" % (b, a, u), w1_rounded[(b, a, u)], 2 * P)
 
         h_ps, h_sb = {}, {}
 
-        def h_pass(b, t, half, a):
+        def h_pass(b, t, bank, a):
             if a == 0:
-                h_ps[(b, t, half)] = psum.tile([P, BANK], F32, name="bank", tag="bank")
+                h_ps[(b, t, bank)] = psum.tile([P, BANK], F32, name="bank", tag="bank")
             codes, scales = w1_q[(b, a, t // 2)]
-            cols = slice(half * BANK, (half + 1) * BANK)
+            rows = slice((t % 2) * P, (t % 2 + 1) * P)
+            cols = slice(bank * BANK, (bank + 1) * BANK)
             nc.tensor.matmul_mx(
-                out=h_ps[(b, t, half)][:],
-                lhsT=codes[:, (t % 2) * P : (t % 2 + 1) * P].bitcast(FP8X4),
-                lhsT_scale=scales[:, (t % 2) * P : (t % 2 + 1) * P],
+                out=h_ps[(b, t, bank)][:],
+                lhsT=codes[:, rows].bitcast(FP8X4),
+                lhsT_scale=scales[:, rows],
                 rhs=v_w[a][:, cols].bitcast(FP8X4),
                 rhs_scale=v_sc[4 * a : P, cols],
                 start=(a == 0),
-                stop=(a == ka - 1),
+                stop=(a == K_PASSES - 1),
             )
 
-        def h_out(b, t, half, engine):
-            if half == 0:
-                h_sb[(b, t)] = ring.tile([P, S], F32, name="h", tag="h", bufs=5, align_bytes=64)
-            copy_on(engine, h_sb[(b, t)][:, half * BANK : (half + 1) * BANK], h_ps[(b, t, half)][:])
+        def h_product(b, t):
+            for bank in range(S // BANK):
+                for a in range(K_PASSES):
+                    h_pass(b, t, bank, a)
 
-        def h_tile_out(b, t):
-            h_out(b, t, 0, "s")
-            h_out(b, t, 1, "s")
+        def h_out(b, t, second_copy=nc.scalar.copy):
+            h_sb[(b, t)] = reused([P, S], F32, "h", PACK + 1)
+            nc.scalar.copy(h_sb[(b, t)][:, 0:BANK], h_ps[(b, t, 0)][:])
+            second_copy(h_sb[(b, t)][:, BANK:S], h_ps[(b, t, 1)][:])
 
-        damp, quot, z_q = {}, {}, {}
+        damp, prod, body = {}, {}, {}
 
-        def picked(b, t, which, m0, w):
-            return h_sb[(b, t)][:].indirect(pos_t[which][:, m0 // 16 : (m0 + w) // 16])
+        def picked(b, t, which, m0, width):
+            return h_sb[(b, t)][:].indirect(pos_t[which][:, m0 // LIST_GROUP : (m0 + width) // LIST_GROUP])
 
-        body = {}
-
-        def rim(b, t, m0, w):
+        def pick_rim(b, t):
             if t == 0:
-                damp[(b, m0)] = keep.tile([P, PACK, w], F32, name="damp%d_%d" % (b, m0), align_bytes=64)
-            nc.vector.tensor_copy(damp[(b, m0)][:, t, :], picked(b, t, 0, m0, w))
+                damp[b] = kept([P, PACK, M], F32, "damp%d" % b)
+            nc.vector.tensor_copy(damp[b][:, t, :], picked(b, t, RIM, 0, M))
 
-        def damping(b, m0, w, t0, t1):
-            x = damp[(b, m0)][:, t0:t1, :]
+        def damping(b, t0, t1, m0, width):
+            x = damp[b][:, t0:t1, m0 : m0 + width]
             nc.scalar.activation(x, x, ACT.Square)
             nc.scalar.activation(x, x, ACT.Abs_reciprocal_sqrt, bias=1.0)
             nc.scalar.activation(x, x, ACT.Square)
 
-        def pick_body(b, t, m0, w):
-            bd = ring.tile([P, w], F32, name="body", tag="body", align_bytes=64)
-            nc.vector.tensor_tensor(bd[:], picked(b, t, 1, m0, w), gain_row[b][:, t, :], MULT)
-            body[(b, t, m0)] = bd
+        def pick_body(b, t, m0, width, dst):
+            nc.vector.tensor_tensor(dst, picked(b, t, BODY, m0, width), gain_rows[b][:, t, 0:width], MULT)
+            body[(b, t, m0)] = dst
 
-        def pick_base(b, t, m0, w):
+        def pick_base(b, t, m0, width):
             if t == 0:
-                quot[(b, m0)] = keep.tile([P, PACK, w], F32, name="quot%d_%d" % (b, m0), align_bytes=64)
-            nc.vector.tensor_tensor(quot[(b, m0)][:, t, :], picked(b, t, 2, m0, w), body[(b, t, m0)][:], MULT)
-
-        z_grp = {}
-
-        def z_round(b, m0, w):
-            zg = grouped(w)
+                prod[b] = kept([P, PACK, M], F32, "prod%d" % b)
             nc.vector.tensor_tensor(
-                zg[:].rearrange("p (c i t) -> p c t i", i=4, t=PACK),
-                quot[(b, m0)][:].rearrange("p t (c i) -> p c t i", i=4),
-                damp[(b, m0)][:].rearrange("p t (c i) -> p c t i", i=4),
+                prod[b][:, t, m0 : m0 + width], picked(b, t, BASE, m0, width), body[(b, t, m0)], MULT
+            )
+
+        def pick_all(b, t):
+            pick_body(b, t, 0, M, reused([P, M], F32, "body", 2)[:])
+            pick_rim(b, t)
+            pick_base(b, t, 0, M)
+
+        z_rounded, z_q = {}, {}
+
+        def round_z(b, m0, width, rounded):
+            nc.vector.tensor_tensor(
+                rounded[:].rearrange("p (c i t) -> p c t i", i=LINE, t=PACK),
+                prod[b][:, :, m0 : m0 + width].rearrange("p t (c i) -> p c t i", i=LINE),
+                damp[b][:, :, m0 : m0 + width].rearrange("p t (c i) -> p c t i", i=LINE),
                 MULT,
             )
-            z_grp[(b, m0)] = zg
+            z_rounded[(b, m0)] = rounded
 
-        def z_quant(b, m0, w):
-            z_q[(b, m0)] = quantize("zq%d_%d" % (b, m0), z_grp[(b, m0)], w)
+        def quantize_z(b, m0, width):
+            z_q[(b, m0)] = quantize("z_%d_%d" % (b, m0), z_rounded[(b, m0)], width)
 
-        wrd_grp, wrd_q = {}, {}
+        wrd_rounded, wrd_q = {}, {}
 
-        def cast_wrd(b, c0, wd, engine):
-            g = grouped(wd)
-            copy_on(
-                engine,
-                g[:].rearrange("p (c i j) -> p c j i", i=4, j=PACK),
-                wrd_raw[(b, c0)][:].rearrange("p j (c i) -> p c j i", i=4),
+        def round_wrd(b, part):
+            width = WRD_PARTS[part][1]
+            rounded = reused([P, PACK * width], BF16, "wide", R_PASSES) if part == 0 else narrow()
+            nc.scalar.copy(
+                rounded[:].rearrange("p (c i j) -> p c j i", i=LINE, j=PACK),
+                wrd_raw[(b, part)][:].rearrange("p j (c i) -> p c j i", i=LINE),
             )
-            wrd_grp[(b, c0)] = g
+            wrd_rounded[(b, part)] = rounded
 
-        def quant_wrd(b, c0, wd):
-            wrd_q[(b, c0)] = quantize("wrdq%d_%d" % (b, c0), wrd_grp[(b, c0)], wd)
+        def quantize_wrd(b, part):
+            wrd_q[(b, part)] = quantize("wrd_%d%d" % (b, part), wrd_rounded[(b, part)], WRD_PARTS[part][1])
 
         y_ps = {}
 
-        def y_pass(b, m0, w, pair):
-            zc, zs = z_q[(0, 0)] if b == 0 else z_q[(1, m0)]
+        def y_pass(b, m0, pair):
+            z_codes, z_scales = z_q[(0, 0)] if b == 0 else z_q[(1, m0)]
             z0 = m0 if b == 0 else 0
-            if b == 0:
-                y_ps[(m0, pair, 0)] = psum.tile([P, BANK], F32, name="bank", tag="bank")
-                y_ps[(m0, pair, 1)] = psum.tile([P, BANK], F32, name="bank", tag="bank")
+            steps = M_HALF // P
             for u in range(2):
                 n0 = (2 * pair + u) * P
-                for s in range(w // P):
+                for s in range(steps):
+                    cols = slice(z0 + s * P, z0 + (s + 1) * P)
                     nc.tensor.matmul_mx(
-                        out=y_ps[(m0, pair, 0)][:, u * w + s * P : u * w + (s + 1) * P],
+                        out=y_ps[(m0, pair, OX)][:, u * M_HALF + s * P : u * M_HALF + (s + 1) * P],
                         lhsT=wox_w[:, b, 2 * n0 : 2 * (n0 + P)].bitcast(FP4X4),
                         lhsT_scale=wox_sc[:, b, n0 : n0 + P],
-                        rhs=zc[:, z0 + s * P : z0 + (s + 1) * P].bitcast(FP8X4),
-                        rhs_scale=zs[:, z0 + s * P : z0 + (s + 1) * P],
+                        rhs=z_codes[:, cols].bitcast(FP8X4),
+                        rhs_scale=z_scales[:, cols],
                         start=(b == 0 and u == 0 and s == 0),
-                        stop=(b == hb - 1 and u == 1 and s == w // P - 1),
+                        stop=(b == R_PASSES - 1 and u == 1 and s == steps - 1),
                     )
             for u in range(2):
                 n0 = (2 * pair + u) * P
-                c0 = 0 if n0 < 512 else 512
-                wc, ws = wrd_q[(b, c0)]
+                part = 0 if n0 < WRD_PARTS[1][0] else 1
+                codes, scales = wrd_q[(b, part)]
+                rows = slice(n0 - WRD_PARTS[part][0], n0 - WRD_PARTS[part][0] + P)
                 nc.tensor.matmul_mx(
-                    out=y_ps[(m0, pair, 1)][:, u * w : (u + 1) * w],
-                    lhsT=wc[:, n0 - c0 : n0 - c0 + P].bitcast(FP8X4),
-                    lhsT_scale=ws[:, n0 - c0 : n0 - c0 + P],
-                    rhs=zc[:, z0 : z0 + w].bitcast(FP8X4),
-                    rhs_scale=zs[:, z0 : z0 + w],
+                    out=y_ps[(m0, pair, RD)][:, u * M_HALF : (u + 1) * M_HALF],
+                    lhsT=codes[:, rows].bitcast(FP8X4),
+                    lhsT_scale=scales[:, rows],
+                    rhs=z_codes[:, z0 : z0 + M_HALF].bitcast(FP8X4),
+                    rhs_scale=z_scales[:, z0 : z0 + M_HALF],
                     start=(b == 0 and u == 0),
-                    stop=(b == hb - 1 and u == 1),
+                    stop=(b == R_PASSES - 1 and u == 1),
                 )
 
-        def y_out(m0, w, pair):
-            ox = ring.tile([P, 2 * w], F32, name="ox", tag="ox", align_bytes=64)
-            nc.scalar.copy(ox[:], y_ps[(m0, pair, 0)][:, 0 : 2 * w])
-            res = ring.tile([P, 2 * w], F32, name="res", tag="res", bufs=4, align_bytes=64)
-            nc.vector.tensor_tensor(res[:], y_ps[(m0, pair, 1)][:, 0 : 2 * w], ox[:], MAX)
+        def y_out(m0, pair):
+            res = reused([P, BANK], F32, "res", 2 * PAIRS)
+            nc.scalar.copy(res[:], y_ps[(m0, pair, OX)][:])
+            nc.vector.tensor_tensor(res[:], y_ps[(m0, pair, RD)][:], res[:], MAX)
             nc.sync.dma_start(
-                out[2 * pair * P : (2 * pair + 2) * P, m0 : m0 + w].rearrange("(u p) m -> p u m", u=2),
+                out[2 * pair * P : (2 * pair + 2) * P, m0 : m0 + M_HALF].rearrange("(u p) m -> p u m", u=2),
                 res[:].rearrange("p (u m) -> p u m", u=2),
             )
 
-        for a in range(ka):
-            cast_w1(0, a, 0, "v")
-            cast_w1(0, a, 1, "s")
-            quant_w1(0, a, 0)
-            for t in range(2):
-                for half in range(2):
-                    h_pass(0, t, half, a)
-            quant_w1(0, a, 1)
-            if a == ka - 1:
-                h_out(0, 0, 0, "s")
-                h_out(0, 0, 1, "v")
-            for t in range(2, PACK):
-                for half in range(2):
-                    h_pass(0, t, half, a)
+        for a in range(K_PASSES):
+            round_w1(0, a, 0, nc.vector.tensor_copy)
+            round_w1(0, a, 1, nc.scalar.copy)
+            for u in range(2):
+                quantize_w1(0, a, u)
+                if a == K_PASSES - 1 and u == 1:
+                    h_out(0, 0, nc.vector.tensor_copy)
+                for t in (2 * u, 2 * u + 1):
+                    for bank in range(S // BANK):
+                        h_pass(0, t, bank, a)
         for t in range(1, PACK):
-            h_tile_out(0, t)
+            h_out(0, t)
         for u in range(2):
-            for a in range(ka):
-                cast_w1(1, a, u, "s")
+            for a in range(K_PASSES):
+                round_w1(1, a, u, nc.scalar.copy)
 
-        def h_tile(b, t):
-            for half in range(2):
-                for a in range(ka):
-                    h_pass(b, t, half, a)
+        pick_all(0, 0)
+        pick_all(0, 1)
+        pick_rim(0, 2)
+        pick_rim(0, 3)
+        for a in range(K_PASSES):
+            quantize_w1(1, a, 0)
+        h_product(1, 0)
+        h_product(1, 1)
+        damping(0, 0, 2, 0, M)
+        h_out(1, 0)
+        h_out(1, 1)
+        pick_body(0, 2, 0, M, turn([P, M], F32, 0)[:])
+        quantize_w1(1, 0, 1)
+        pick_base(0, 2, 0, M)
+        for a in range(1, K_PASSES):
+            quantize_w1(1, a, 1)
+        h_product(1, 2)
+        h_product(1, 3)
+        h_out(1, 2)
+        h_out(1, 3)
+        pick_body(0, 3, 0, M, turn([P, M], F32, 1)[:])
+        pick_base(0, 3, 0, M)
+        damping(0, 2, PACK, 0, M)
 
-        def picks(b, t, m0, w):
-            pick_body(b, t, m0, w)
-            rim(b, t, m0, w)
-            pick_base(b, t, m0, w)
+        for part in range(len(WRD_PARTS)):
+            round_wrd(0, part)
+        for t in range(LAST):
+            pick_all(1, t)
+        for part in range(len(WRD_PARTS)):
+            round_wrd(1, part)
 
-        W = 256
-        picks(0, 0, 0, M)
-        picks(0, 1, 0, M)
-        for a in range(ka):
-            quant_w1(1, a, 0)
-        h_tile(1, 0)
-        h_tile(1, 1)
-        h_tile_out(1, 0)
-        h_tile_out(1, 1)
-        picks(0, 2, 0, M)
-        for a in range(ka):
-            quant_w1(1, a, 1)
-        h_tile(1, 2)
-        h_tile(1, 3)
-        damping(0, 0, M, 0, 2)
-        h_tile_out(1, 2)
-        h_tile_out(1, 3)
-        picks(0, 3, 0, M)
-        damping(0, 0, M, 2, 4)
-        cast_wrd(0, 0, 512, "s")
-        cast_wrd(0, 512, 256, "s")
-        for t in range(PACK):
-            picks(1, t, 0, W)
-        damping(1, 0, W, 0, 4)
-        z_round(0, 0, M)
-        for t in range(PACK):
-            rim(1, t, W, W)
-        z_quant(0, 0, M)
-        cast_wrd(1, 0, 512, "s")
-        cast_wrd(1, 512, 256, "s")
-        damping(1, W, W, 0, 4)
-        quant_wrd(0, 0, 512)
-        quant_wrd(0, 512, 256)
-        for pair in range(3):
-            y_pass(0, 0, W, pair)
-        pick_body(1, 0, W, W)
-        pick_body(1, 1, W, W)
-        pick_base(1, 0, W, W)
-        z_round(1, 0, W)
-        pick_base(1, 1, W, W)
-        z_quant(1, 0, W)
-        pick_body(1, 2, W, W)
-        pick_body(1, 3, W, W)
-        quant_wrd(1, 0, 512)
-        quant_wrd(1, 512, 256)
-        for pair in range(3):
-            y_pass(1, 0, W, pair)
-        pick_base(1, 2, W, W)
-        pick_base(1, 3, W, W)
-        y_out(0, W, 0)
-        z_round(1, W, W)
-        y_pass(0, W, W, 0)
-        y_out(0, W, 1)
-        z_quant(1, W, W)
-        y_pass(0, W, W, 1)
-        y_out(0, W, 2)
-        y_pass(0, W, W, 2)
-        for pair in range(3):
-            y_pass(1, W, W, pair)
-            y_out(W, W, pair)
+        round_z(0, 0, M, reused([P, PACK * M], BF16, "gain_rows0", 1))
+        pick_rim(1, LAST)
+        quantize_z(0, 0, M)
+        pick_body(1, LAST, 0, M_HALF, reused([P, M_HALF], F32, "gain_rows0", 1)[:])
+        quantize_wrd(0, 0)
+        pick_base(1, LAST, 0, M_HALF)
+        quantize_wrd(0, 1)
+        damping(1, 0, 2, 0, M)
+        damping(1, 2, PACK, 0, M_HALF)
+        damping(1, 2, PACK, M_HALF, M_HALF)
+
+        first_banks = [(0, pair, style) for style in (OX, RD) for pair in range(PAIRS)]
+        second_banks = [(M_HALF, pair, style) for pair in range(PAIRS) for style in (OX, RD)]
+        for key in first_banks + second_banks:
+            y_ps[key] = psum.tile([P, BANK], F32, name="bank", tag="bank")
+        for pair in range(PAIRS):
+            y_pass(0, 0, pair)
+        y_pass(0, M_HALF, 0)
+        for part in range(len(WRD_PARTS)):
+            quantize_wrd(1, part)
+
+        round_z(1, 0, M_HALF, turn([P, PACK * M_HALF], BF16, 0))
+        pick_body(1, LAST, M_HALF, M_HALF, damp[1][:, 0, 0:M_HALF])
+        quantize_z(1, 0, M_HALF)
+        pick_base(1, LAST, M_HALF, M_HALF)
+        for pair in range(PAIRS):
+            y_pass(1, 0, pair)
+        y_out(0, 0)
+        round_z(1, M_HALF, M_HALF, turn([P, PACK * M_HALF], BF16, 1))
+        quantize_z(1, M_HALF, M_HALF)
+        for pair in range(1, PAIRS):
+            y_pass(0, M_HALF, pair)
+            y_out(0, pair)
+        for pair in range(PAIRS):
+            y_pass(1, M_HALF, pair)
+            y_out(M_HALF, pair)

@@ -15,6 +15,7 @@ FP8X4 = mybir.dt.float8_e4m3fn_x4
 FP4X4 = mybir.dt.float4_e2m1fn_x4
 ACT = mybir.ActivationFunctionType
 MULT = mybir.AluOpType.mult
+ADD = mybir.AluOpType.add
 MAX = mybir.AluOpType.max
 
 P = 128
@@ -28,7 +29,6 @@ BANK = 512
 LINE = 4
 M_HALF = M // 2
 PAIRS = N // (2 * P)
-WRD_PARTS = ((0, 512), (512, 256))
 RIM, BODY, BASE = 0, 1, 2
 OX, RD = 0, 1
 LAST = PACK - 1
@@ -40,196 +40,284 @@ def tile_list_sherd_vessel_joining_kernel(
     nc = tc.nc
     with ExitStack() as ctx:
         keep = ctx.enter_context(tc.tile_pool(name="keep", bufs=1))
-        ring = ctx.enter_context(tc.tile_pool(name="ring", bufs=2))
+        ring = ctx.enter_context(tc.tile_pool(name="ring", bufs=PACK + 1))
+        shared = ctx.enter_context(tc.tile_pool(name="shared", bufs=1))
         psum = ctx.enter_context(tc.psum_pool(name="psum", bufs=8))
 
         def kept(shape, dtype, name):
             return keep.tile(shape, dtype, name=name, align_bytes=64)
 
-        def reused(shape, dtype, tag, bufs):
-            return ring.tile(shape, dtype, name=tag, tag=tag, bufs=bufs, align_bytes=64)
+        def placed(shape, dtype, name, kib):
+            return shared.tile(shape, dtype, name=name, align_bytes=64, offset=int(1024 * kib))
 
-        def load_rows(src, row0, col0, width):
-            raw = reused([P, PACK, width], F32, "raw", 4)
-            rows = src[row0 : row0 + PASS, col0 : col0 + width]
+        def load_rows(src, name, a, col0, width, kib):
+            raw = placed([P, PACK, width], F32, name, kib)
+            rows = src[a * PASS : (a + 1) * PASS, col0 : col0 + width]
             nc.sync.dma_start(raw[:], rows.rearrange("(p j) c -> p j c", j=PACK))
             return raw
 
-        offs_t = keep.tile([P, S // LIST_GROUP], U16, name="offs_t")
-        nc.sync.dma_start(offs_t[:], offs)
+        def load_list(entries, name):
+            tile = keep.tile(list(entries.shape), U16, name=name)
+            nc.sync.dma_start(tile[:], entries)
+            return tile
 
+        def load_table(a, kib):
+            words = placed([P, T], U32, "tab_w%d" % a, kib)
+            nc.sync.dma_start(words[:].bitcast(I32), tab_words[a].rearrange("p t i -> p (t i)").bitcast(I32))
+            return words
+
+        offs_t = load_list(offs, "offs_t")
         tab_sc = kept([P, T], U8, "tab_sc")
         wox_sc = kept([P, R_PASSES, N], U8, "wox_sc")
         nc.vector.memset(tab_sc[:].bitcast(I32), 0)
         nc.vector.memset(wox_sc[:].rearrange("p b n -> p (b n)").bitcast(I32), 0)
 
-        w1_raw, tab_w = {}, []
-        for a in range(K_PASSES):
-            words = kept([P, T], U32, "tab_w%d" % a)
-            nc.sync.dma_start(words[:].bitcast(I32), tab_words[a].rearrange("p t i -> p (t i)").bitcast(I32))
-            tab_w.append(words)
-            if a == 0:
-                for q in range(QUADRANTS):
-                    nc.sync.dma_start(
-                        tab_sc[32 * q : 32 * q + 4 * K_PASSES, :].bitcast(I32),
-                        tab_scales[:, 4 * q : 4 * q + 4, :].bitcast(I32),
-                    )
-            w1_raw[(0, a)] = load_rows(w1, a * PASS, 0, PASS)
-
-        gain_t = keep.tile([P, R_PASSES, PACK], F32, name="gain_t")
-        nc.gpsimd.dma_start(gain_t[:], gain.rearrange("(b p t) -> p b t", b=R_PASSES, t=PACK))
-        gain_rows = []
-        for b in range(R_PASSES):
-            rows = reused([P, PACK, M], F32, "gain_rows%d" % b, 1)
-            nc.scalar.activation(rows[:], gain_t[:, b, :].unsqueeze(2).to_broadcast([P, PACK, M]), ACT.Copy)
-            gain_rows.append(rows)
+        raw, tab_w = {}, {}
+        tab_w[0] = load_table(0, 0)
         for q in range(QUADRANTS):
-            nc.gpsimd.dma_start(
-                wox_sc[32 * q : 32 * q + 4, :, :].bitcast(I32),
-                wox_scales[:, 4 * q : 4 * q + 4, :].rearrange("b r n -> r b n").bitcast(I32),
+            nc.sync.dma_start(
+                tab_sc[32 * q : 32 * q + 4 * K_PASSES, :].bitcast(I32),
+                tab_scales[:, 4 * q : 4 * q + 4, :].bitcast(I32),
             )
-
-        pos_t = []
-        for which, pos in enumerate((pos1, pos2, pos3)):
-            entries = keep.tile([P, M // LIST_GROUP], U16, name="pos_t%d" % which)
-            nc.sync.dma_start(entries[:], pos)
-            pos_t.append(entries)
         for a in range(K_PASSES):
-            w1_raw[(1, a)] = load_rows(w1, a * PASS, PASS, PASS)
-        wox_w = kept([P, R_PASSES, 2 * N], U8, "wox_w")
-        nc.sync.dma_start(wox_w[:].bitcast(I32), wox_words.rearrange("b p c -> p b c").bitcast(I32))
-        wrd_raw = {}
+            if a > 0:
+                tab_w[a] = load_table(a, (0, 32, 16)[a])
+            raw[(0, a)] = load_rows(w1, "w1_0%d" % a, a, 0, PASS, 48 + 8 * a)
+        pos_t = [load_list(pos, "pos_t%d" % which) for which, pos in enumerate((pos1, pos2, pos3))]
+        for a in range(K_PASSES):
+            raw[(1, a)] = load_rows(w1, "w1_1%d" % a, a, PASS, PASS, 72 + 8 * a)
+
+        gain_t = keep.tile([P, R_PASSES * PACK], F32, name="gain_t")
+        nc.gpsimd.dma_start(
+            gain_t[:].rearrange("p (b t) -> p b t", t=PACK), gain.rearrange("(b p t) -> p b t", b=R_PASSES, t=PACK)
+        )
+        warm = keep.tile([P, 1], F32, name="warm")
+        nc.scalar.activation(warm[:], gain_t[:, 0:1], ACT.Abs_reciprocal_sqrt, bias=1.0, scale=0.0)
+        gain_rows = kept([P, R_PASSES * PACK, M], F32, "gain_rows")
         for b in range(R_PASSES):
-            for part, (col0, width) in enumerate(WRD_PARTS):
-                wrd_raw[(b, part)] = load_rows(wrd, b * PASS, col0, width)
+            some = slice(b * PACK, (b + 1) * PACK)
+            nc.scalar.activation(gain_rows[:, some, :], gain_t[:, some].unsqueeze(2).to_broadcast([P, PACK, M]), ACT.Copy)
 
-        v_w = []
+        v_w = [kept([P, S], U32, "v_w%d" % a) for a in range(K_PASSES)]
         v_sc = kept([P, S], U8, "v_sc")
-        for a in range(K_PASSES):
-            words = kept([P, S], U32, "v_w%d" % a)
-            nc.vector.tensor_copy(words[:], tab_w[a][:].indirect(offs_t[:]))
-            v_w.append(words)
-            if a == 0:
-                nc.vector.tensor_copy(v_sc[:], tab_sc[:].indirect(offs_t[:]))
 
-        def quantize(name, rounded, width):
-            codes = kept([P, width], U32, name + "_codes")
+        def gather_words(a, j0, width):
+            entries = offs_t[:, j0 // LIST_GROUP : (j0 + width) // LIST_GROUP]
+            nc.vector.tensor_copy(v_w[a][:, j0 : j0 + width], tab_w[a][:].indirect(entries))
+
+        def quantize(name, rounded, codes=None):
+            width = rounded.shape[1] // PACK
             scales = kept([P, width], U8, name + "_scales")
-            nc.vector.quantize_mx(out=codes[:].bitcast(FP8X4), scales=scales[:], in_=rounded[:])
+            if codes is None:
+                codes = kept([P, width], U32, name + "_codes")
+            nc.vector.quantize_mx(out=codes[:].bitcast(FP8X4), scales=scales[:], in_=rounded)
             return codes, scales
 
-        def turn(shape, dtype, u):
-            return reused(shape, dtype, "turn%d" % u, 1)
+        def blocks(pair):
+            codes, scales = pair
+            return [(codes[:, c : c + P], scales[:, c : c + P]) for c in range(0, codes.shape[1], P)]
 
-        def narrow():
-            return reused([P, 2 * P * PACK], BF16, "narrow", 4)
+        def scalar_round(dst, src):
+            nc.scalar.copy(
+                dst.rearrange("p (c i j) -> p c j i", i=LINE, j=PACK), src.rearrange("p j (c i) -> p c j i", i=LINE)
+            )
 
-        w1_rounded, w1_q = {}, {}
+        def gpsimd_round(dst, src):
+            nc.gpsimd.tensor_scalar(
+                dst.rearrange("p (c j) -> p c j", j=PACK), src.rearrange("p j c -> p c j"), 1.0, 0.0, MULT, ADD
+            )
 
-        def round_w1(b, a, u, copy):
-            rounded = turn([P, 2 * P * PACK], BF16, u) if (b, a) == (1, K_PASSES - 1) else narrow()
-            src = w1_raw[(b, a)][:].rearrange("p j (m t) -> p m j t", t=PACK)
-            copy(rounded[:].rearrange("p (s m j) -> p m j s", s=2, j=PACK), src[:, :, :, 2 * u : 2 * u + 2])
-            w1_rounded[(b, a, u)] = rounded
+        def round_w1(b, a, u, dst, copy=nc.scalar.copy):
+            src = raw[(b, a)][:].rearrange("p j (m t) -> p m j t", t=PACK)
+            copy(dst.rearrange("p (s m j) -> p m j s", s=2, j=PACK), src[:, :, :, 2 * u : 2 * u + 2])
 
-        def quantize_w1(b, a, u):
-            w1_q[(b, a, u)] = quantize("w1_%d%d%d" % (b, a, u), w1_rounded[(b, a, u)], 2 * P)
+        w1_q, h_ps, h_sb = {}, {}, {}
 
-        h_ps, h_sb = {}, {}
+        def quantize_w1(name, rounded, passes, tiles, codes=None):
+            made = blocks(quantize(name, rounded, codes))
+            for n, key in enumerate([(g, a) for a in passes for g in tiles]):
+                w1_q[key] = made[n]
 
-        def h_pass(b, t, bank, a):
+        def h_pass(g, bank, a):
             if a == 0:
-                h_ps[(b, t, bank)] = psum.tile([P, BANK], F32, name="bank", tag="bank")
-            codes, scales = w1_q[(b, a, t // 2)]
-            rows = slice((t % 2) * P, (t % 2 + 1) * P)
+                h_ps[(g, bank)] = psum.tile([P, BANK], F32, name="bank", tag="bank")
+            codes, scales = w1_q[(g, a)]
             cols = slice(bank * BANK, (bank + 1) * BANK)
             nc.tensor.matmul_mx(
-                out=h_ps[(b, t, bank)][:],
-                lhsT=codes[:, rows].bitcast(FP8X4),
-                lhsT_scale=scales[:, rows],
+                out=h_ps[(g, bank)][:],
+                lhsT=codes.bitcast(FP8X4),
+                lhsT_scale=scales,
                 rhs=v_w[a][:, cols].bitcast(FP8X4),
                 rhs_scale=v_sc[4 * a : P, cols],
                 start=(a == 0),
                 stop=(a == K_PASSES - 1),
             )
 
-        def h_product(b, t):
-            for bank in range(S // BANK):
-                for a in range(K_PASSES):
-                    h_pass(b, t, bank, a)
+        def h_product(tiles):
+            for g in tiles:
+                for bank in range(S // BANK):
+                    for a in range(K_PASSES):
+                        h_pass(g, bank, a)
 
-        def h_out(b, t, second_copy=nc.scalar.copy):
-            h_sb[(b, t)] = reused([P, S], F32, "h", PACK + 1)
-            nc.scalar.copy(h_sb[(b, t)][:, 0:BANK], h_ps[(b, t, 0)][:])
-            second_copy(h_sb[(b, t)][:, BANK:S], h_ps[(b, t, 1)][:])
+        def h_out(g, tile=None, second_copy=nc.scalar.copy):
+            h_sb[g] = ring.tile([P, S], F32, name="h", tag="h", align_bytes=64) if tile is None else tile
+            nc.scalar.copy(h_sb[g][:, 0:BANK], h_ps[(g, 0)][:])
+            second_copy(h_sb[g][:, BANK:S], h_ps[(g, 1)][:])
 
-        damp, prod, body = {}, {}, {}
+        def picked(g, which, m0, width):
+            return h_sb[g][:].indirect(pos_t[which][:, m0 // LIST_GROUP : (m0 + width) // LIST_GROUP])
 
-        def picked(b, t, which, m0, width):
-            return h_sb[(b, t)][:].indirect(pos_t[which][:, m0 // LIST_GROUP : (m0 + width) // LIST_GROUP])
+        def square(dst, src):
+            nc.scalar.activation(dst, src, ACT.Square)
 
-        def pick_rim(b, t):
-            if t == 0:
-                damp[b] = kept([P, PACK, M], F32, "damp%d" % b)
-            nc.vector.tensor_copy(damp[b][:, t, :], picked(b, t, RIM, 0, M))
+        def inverse_root(dst, src):
+            nc.scalar.activation(dst, src, ACT.Abs_reciprocal_sqrt, bias=1.0)
 
-        def damping(b, t0, t1, m0, width):
-            x = damp[b][:, t0:t1, m0 : m0 + width]
-            nc.scalar.activation(x, x, ACT.Square)
-            nc.scalar.activation(x, x, ACT.Abs_reciprocal_sqrt, bias=1.0)
-            nc.scalar.activation(x, x, ACT.Square)
 
-        def pick_body(b, t, m0, width, dst):
-            nc.vector.tensor_tensor(dst, picked(b, t, BODY, m0, width), gain_rows[b][:, t, 0:width], MULT)
-            body[(b, t, m0)] = dst
-
-        def pick_base(b, t, m0, width):
-            if t == 0:
-                prod[b] = kept([P, PACK, M], F32, "prod%d" % b)
-            nc.vector.tensor_tensor(
-                prod[b][:, t, m0 : m0 + width], picked(b, t, BASE, m0, width), body[(b, t, m0)], MULT
+        for a in range(K_PASSES):
+            gather_words(a, 0, S)
+            if a == 0:
+                nc.vector.tensor_copy(v_sc[:], tab_sc[:].indirect(offs_t[:]))
+            for u in range(2):
+                rounded = ring.tile([P, 2 * PACK * P], BF16, name="narrow", tag="narrow", bufs=4, align_bytes=64)
+                round_w1(0, a, u, rounded[:], (nc.vector.tensor_copy, nc.scalar.copy)[u])
+                codes = placed([P, 2 * P], U32, "first_codes%d" % u, 33.5 + 6 * u) if a == K_PASSES - 1 else None
+                quantize_w1("w1_0%d%d" % (a, u), rounded[:], [a], [2 * u, 2 * u + 1], codes)
+            for g in range(PACK):
+                for bank in range(S // BANK):
+                    h_pass(g, bank, a)
+        wrd_raw = [load_rows(wrd, "wrd_raw%d" % b, b, 0, N, 8 + 12 * b) for b in range(R_PASSES)]
+        wox_w = kept([P, R_PASSES, 2 * N], U8, "wox_w")
+        nc.sync.dma_start(wox_w[:].bitcast(I32), wox_words.rearrange("b p c -> p b c").bitcast(I32))
+        for q in range(QUADRANTS):
+            nc.sync.dma_start(
+                wox_sc[32 * q : 32 * q + 4, :, :].bitcast(I32),
+                wox_scales[:, 4 * q : 4 * q + 4, :].rearrange("b r n -> r b n").bitcast(I32),
             )
 
-        def pick_all(b, t):
-            pick_body(b, t, 0, M, reused([P, M], F32, "body", 2)[:])
-            pick_rim(b, t)
-            pick_base(b, t, 0, M)
+        late_first = [placed([P, 2, 2 * PACK * P], BF16, "late_first%d" % u, 34 + 6 * u) for u in range(2)]
+        late_last = [placed([P, 2 * PACK * P], BF16, "late_last%d" % u, 38 + 6 * u) for u in range(2)]
 
-        z_rounded, z_q = {}, {}
+        def round_late(a, u):
+            round_w1(1, a, u, late_first[u][:, a, :] if a < 2 else late_last[u][:])
+
+        def quantize_late(u):
+            tiles = [PACK + 2 * u, PACK + 2 * u + 1]
+            quantize_w1("late_first%d" % u, late_first[u][:].rearrange("p a c -> p (a c)"), [0, 1], tiles)
+            quantize_w1("late_last%d" % u, late_last[u][:], [2], tiles)
+            h_product(tiles)
+
+        h_out(0, second_copy=nc.vector.tensor_copy)
+        h_out(1)
+        round_late(0, 0)
+        round_late(1, 0)
+        h_out(2)
+        round_late(2, 0)
+        round_late(0, 1)
+        h_out(3)
+        round_late(1, 1)
+        round_late(2, 1)
+
+        prod = [placed([P, PACK, M], F32, "prod%d" % b, (56, 80)[b]) for b in range(R_PASSES)]
+        damp = [placed([P, PACK, M], F32, "damp%d" % b, (48, 64)[b]) for b in range(R_PASSES)]
+        body, z_rounded, z_q = {}, {}, {}
+
+        def pick_body(g, m0, width, dst):
+            nc.vector.tensor_tensor(dst, picked(g, BODY, m0, width), gain_rows[:, g, 0:width], MULT)
+            body[(g, m0)] = dst
+
+        def pick_rim(g, dst):
+            nc.vector.tensor_copy(dst, picked(g, RIM, 0, M))
+
+        def pick_base(g, m0, width):
+            dst = prod[g // PACK][:, g % PACK, m0 : m0 + width]
+            nc.vector.tensor_tensor(dst, picked(g, BASE, m0, width), body[(g, m0)], MULT)
+
+        def pick_all(g, body_dst, rim_dst):
+            pick_body(g, 0, M, body_dst)
+            pick_rim(g, rim_dst)
+            pick_base(g, 0, M)
+
+        def body_buffer():
+            return ring.tile([P, M], F32, name="body", tag="body", bufs=2, align_bytes=64)[:]
 
         def round_z(b, m0, width, rounded):
             nc.vector.tensor_tensor(
-                rounded[:].rearrange("p (c i t) -> p c t i", i=LINE, t=PACK),
+                rounded.rearrange("p (c i t) -> p c t i", i=LINE, t=PACK),
                 prod[b][:, :, m0 : m0 + width].rearrange("p t (c i) -> p c t i", i=LINE),
                 damp[b][:, :, m0 : m0 + width].rearrange("p t (c i) -> p c t i", i=LINE),
                 MULT,
             )
-            z_rounded[(b, m0)] = rounded
 
-        def quantize_z(b, m0, width):
-            z_q[(b, m0)] = quantize("z_%d_%d" % (b, m0), z_rounded[(b, m0)], width)
+        def quantize_z(b, m0, codes=None):
+            z_q[(b, m0)] = quantize("z_%d_%d" % (b, m0), z_rounded[(b, m0)][:], codes)
 
-        wrd_rounded, wrd_q = {}, {}
+        for g in range(2):
+            pick_all(g, body_buffer(), damp[0][:, g, :])
+        rims = []
+        for u in range(2):
+            quantize_late(u)
+            rims.append(placed([P, M], F32, "rim%d" % (2 + u), 74 + 16 * u))
+            pick_all(2 + u, placed([P, M], F32, "body%d" % (2 + u), 72 + 16 * u)[:], rims[u][:])
+        square(damp[0][:, 0:2, :], damp[0][:, 0:2, :])
+        h_out(4)
+        h_out(5)
+        inverse_root(damp[0][:, 0:2, :], damp[0][:, 0:2, :])
+        for u in range(2):
+            square(damp[0][:, 2 + u, :], rims[u][:])
+        square(damp[0][:, 0:2, :], damp[0][:, 0:2, :])
+        roots = placed([P, 2, M], F32, "roots", 94)
+        inverse_root(roots[:], damp[0][:, 2:PACK, :])
+        h_out(6)
+        h_out(7)
+        square(damp[0][:, 2:PACK, :], roots[:])
+        wrd0_rounded = placed([P, PACK * N], BF16, "wrd0_rounded", 34)
+        scalar_round(wrd0_rounded[:], wrd_raw[0][:])
+        wrd1_rounded = placed([P, PACK * PASS], BF16, "wrd1_rounded", 40)
 
-        def round_wrd(b, part):
-            width = WRD_PARTS[part][1]
-            rounded = reused([P, PACK * width], BF16, "wide", R_PASSES) if part == 0 else narrow()
-            nc.scalar.copy(
-                rounded[:].rearrange("p (c i j) -> p c j i", i=LINE, j=PACK),
-                wrd_raw[(b, part)][:].rearrange("p j (c i) -> p c j i", i=LINE),
-            )
-            wrd_rounded[(b, part)] = rounded
+        for g in range(PACK, PACK + 2):
+            pick_all(g, body_buffer(), damp[1][:, g - PACK, :])
+        z_rounded[(0, 0)] = placed([P, PACK * M], BF16, "z_rounded0", 100)
+        round_z(0, 0, M_HALF, z_rounded[(0, 0)][:, 0 : PACK * M_HALF])
+        pick_body(6, 0, M, placed([P, M], F32, "body6", 92.5)[:])
+        round_z(0, M_HALF, M_HALF, z_rounded[(0, 0)][:, PACK * M_HALF : PACK * M])
+        pick_base(6, 0, M)
+        rims = [placed([P, M], F32, "rim%d" % (6 + u), 94.5 + 2 * u) for u in range(2)]
+        for u in range(2):
+            pick_rim(6 + u, rims[u][:])
+        wrd1_front = placed([P, PACK * (N - PASS)], BF16, "wrd1_front", 92.5)
+        gpsimd_round(wrd1_front[:], wrd_raw[1][:, :, 0 : N - PASS])
+        x = damp[1][:, 0:2, :]
+        square(x, x)
+        scalar_round(wrd1_rounded[:, 0 : 2 * PACK * P], wrd_raw[1][:, :, 2 * P : 4 * P])
+        inverse_root(x, x)
+        scalar_round(wrd1_rounded[:, 2 * PACK * P : 4 * PACK * P], wrd_raw[1][:, :, 4 * P : N])
+        square(x, x)
+        halves = [damp[1][:, 2:PACK, m0 : m0 + M_HALF] for m0 in (0, M_HALF)]
+        half_roots = placed([P, 2, M_HALF], F32, "half_roots", 108)
+        for u in range(2):
+            square(damp[1][:, 2 + u, :], rims[u][:])
+        inverse_root(half_roots[:], halves[0])
+        inverse_root(halves[1], halves[1])
+        square(halves[0], half_roots[:])
+        square(halves[1], halves[1])
 
-        def quantize_wrd(b, part):
-            wrd_q[(b, part)] = quantize("wrd_%d%d" % (b, part), wrd_rounded[(b, part)], WRD_PARTS[part][1])
+        wrd_q = [[], []]
+        wrd_q[0].extend(blocks(quantize("wrd_0a", wrd0_rounded[:, 0 : PACK * PASS])))
+        wrd_q[0].extend(blocks(quantize("wrd_0b", wrd0_rounded[:, PACK * PASS : PACK * N])))
+        quantize_z(0, 0, placed([P, M], U32, "z0_codes", 20))
+        pick_body(7, 0, M_HALF, placed([P, M_HALF], F32, "last_body", 22)[:])
+        wrd_q[1].extend(blocks(quantize("wrd_1a", wrd1_front[:])))
+        pick_base(7, 0, M_HALF)
+        wrd_q[1].extend(blocks(quantize("wrd_1b", wrd1_rounded[:])))
 
         y_ps = {}
 
-        def y_pass(b, m0, pair):
+        def y_pass(b, m0, pair, style):
             z_codes, z_scales = z_q[(0, 0)] if b == 0 else z_q[(1, m0)]
             z0 = m0 if b == 0 else 0
             steps = M_HALF // P
-            for u in range(2):
+            for u in range(2 if style == OX else 0):
                 n0 = (2 * pair + u) * P
                 for s in range(steps):
                     cols = slice(z0 + s * P, z0 + (s + 1) * P)
@@ -242,15 +330,12 @@ def tile_list_sherd_vessel_joining_kernel(
                         start=(b == 0 and u == 0 and s == 0),
                         stop=(b == R_PASSES - 1 and u == 1 and s == steps - 1),
                     )
-            for u in range(2):
-                n0 = (2 * pair + u) * P
-                part = 0 if n0 < WRD_PARTS[1][0] else 1
-                codes, scales = wrd_q[(b, part)]
-                rows = slice(n0 - WRD_PARTS[part][0], n0 - WRD_PARTS[part][0] + P)
+            for u in range(2 if style == RD else 0):
+                codes, scales = wrd_q[b][2 * pair + u]
                 nc.tensor.matmul_mx(
                     out=y_ps[(m0, pair, RD)][:, u * M_HALF : (u + 1) * M_HALF],
-                    lhsT=codes[:, rows].bitcast(FP8X4),
-                    lhsT_scale=scales[:, rows],
+                    lhsT=codes.bitcast(FP8X4),
+                    lhsT_scale=scales,
                     rhs=z_codes[:, z0 : z0 + M_HALF].bitcast(FP8X4),
                     rhs_scale=z_scales[:, z0 : z0 + M_HALF],
                     start=(b == 0 and u == 0),
@@ -258,7 +343,7 @@ def tile_list_sherd_vessel_joining_kernel(
                 )
 
         def y_out(m0, pair):
-            res = reused([P, BANK], F32, "res", 2 * PAIRS)
+            res = placed([P, BANK], F32, "res_%d_%d" % (m0, pair), 8 + 2 * (PAIRS * (m0 // M_HALF) + pair))
             nc.scalar.copy(res[:], y_ps[(m0, pair, OX)][:])
             nc.vector.tensor_tensor(res[:], y_ps[(m0, pair, RD)][:], res[:], MAX)
             nc.sync.dma_start(
@@ -266,86 +351,36 @@ def tile_list_sherd_vessel_joining_kernel(
                 res[:].rearrange("p (u m) -> p u m", u=2),
             )
 
-        for a in range(K_PASSES):
-            round_w1(0, a, 0, nc.vector.tensor_copy)
-            round_w1(0, a, 1, nc.scalar.copy)
-            for u in range(2):
-                quantize_w1(0, a, u)
-                if a == K_PASSES - 1 and u == 1:
-                    h_out(0, 0, nc.vector.tensor_copy)
-                for t in (2 * u, 2 * u + 1):
-                    for bank in range(S // BANK):
-                        h_pass(0, t, bank, a)
-        for t in range(1, PACK):
-            h_out(0, t)
-        for u in range(2):
-            for a in range(K_PASSES):
-                round_w1(1, a, u, nc.scalar.copy)
-
-        pick_all(0, 0)
-        pick_all(0, 1)
-        pick_rim(0, 2)
-        pick_rim(0, 3)
-        for a in range(K_PASSES):
-            quantize_w1(1, a, 0)
-        h_product(1, 0)
-        h_product(1, 1)
-        damping(0, 0, 2, 0, M)
-        h_out(1, 0)
-        h_out(1, 1)
-        pick_body(0, 2, 0, M, turn([P, M], F32, 0)[:])
-        quantize_w1(1, 0, 1)
-        pick_base(0, 2, 0, M)
-        for a in range(1, K_PASSES):
-            quantize_w1(1, a, 1)
-        h_product(1, 2)
-        h_product(1, 3)
-        h_out(1, 2)
-        h_out(1, 3)
-        pick_body(0, 3, 0, M, turn([P, M], F32, 1)[:])
-        pick_base(0, 3, 0, M)
-        damping(0, 2, PACK, 0, M)
-
-        for part in range(len(WRD_PARTS)):
-            round_wrd(0, part)
-        for t in range(LAST):
-            pick_all(1, t)
-        for part in range(len(WRD_PARTS)):
-            round_wrd(1, part)
-
-        round_z(0, 0, M, reused([P, PACK * M], BF16, "gain_rows0", 1))
-        pick_rim(1, LAST)
-        quantize_z(0, 0, M)
-        pick_body(1, LAST, 0, M_HALF, reused([P, M_HALF], F32, "gain_rows0", 1)[:])
-        quantize_wrd(0, 0)
-        pick_base(1, LAST, 0, M_HALF)
-        quantize_wrd(0, 1)
-        damping(1, 0, 2, 0, M)
-        damping(1, 2, PACK, 0, M_HALF)
-        damping(1, 2, PACK, M_HALF, M_HALF)
-
         first_banks = [(0, pair, style) for style in (OX, RD) for pair in range(PAIRS)]
         second_banks = [(M_HALF, pair, style) for pair in range(PAIRS) for style in (OX, RD)]
         for key in first_banks + second_banks:
             y_ps[key] = psum.tile([P, BANK], F32, name="bank", tag="bank")
         for pair in range(PAIRS):
-            y_pass(0, 0, pair)
-        y_pass(0, M_HALF, 0)
-        for part in range(len(WRD_PARTS)):
-            quantize_wrd(1, part)
+            y_pass(0, 0, pair, OX)
+        y_pass(0, M_HALF, 0, OX)
+        for pair in range(PAIRS):
+            y_pass(0, 0, pair, RD)
+        y_pass(0, M_HALF, 0, RD)
 
-        round_z(1, 0, M_HALF, turn([P, PACK * M_HALF], BF16, 0))
-        pick_body(1, LAST, M_HALF, M_HALF, damp[1][:, 0, 0:M_HALF])
-        quantize_z(1, 0, M_HALF)
-        pick_base(1, LAST, M_HALF, M_HALF)
-        for pair in range(PAIRS):
-            y_pass(1, 0, pair)
+        for m0 in (0, M_HALF):
+            z_rounded[(1, m0)] = placed([P, PACK * M_HALF], BF16, "z_rounded1_%d" % m0, 104 + 2 * (m0 // M_HALF))
+        round_z(1, 0, M_HALF, z_rounded[(1, 0)][:])
+        pick_body(7, M_HALF, M_HALF, placed([P, M_HALF], F32, "last_body2", 108)[:])
+        quantize_z(1, 0)
+        pick_base(7, M_HALF, M_HALF)
+        last_order = ((0, OX), (1, OX), (0, RD), (2, OX), (1, RD), (2, RD))
+        for pair, style in last_order:
+            y_pass(1, 0, pair, style)
+        round_z(1, M_HALF, M_HALF, z_rounded[(1, M_HALF)][:])
         y_out(0, 0)
-        round_z(1, M_HALF, M_HALF, turn([P, PACK * M_HALF], BF16, 1))
-        quantize_z(1, M_HALF, M_HALF)
+        quantize_z(1, M_HALF)
         for pair in range(1, PAIRS):
-            y_pass(0, M_HALF, pair)
             y_out(0, pair)
+        for style in (OX, RD):
+            y_pass(0, M_HALF, 1, style)
+        for pair, style in last_order:
+            if pair == PAIRS - 1:
+                y_pass(0, M_HALF, pair, style)
+            y_pass(1, M_HALF, pair, style)
         for pair in range(PAIRS):
-            y_pass(1, M_HALF, pair)
             y_out(M_HALF, pair)

@@ -31,6 +31,7 @@ M_HALF = M // 2
 PAIRS = N // (2 * P)
 RIM, BODY, BASE = 0, 1, 2
 OX, RD = 0, 1
+SHARE = 224
 LAST = PACK - 1
 
 
@@ -66,7 +67,6 @@ def tile_list_sherd_vessel_joining_kernel(
             nc.sync.dma_start(words[:].bitcast(I32), tab_words[a].rearrange("p t i -> p (t i)").bitcast(I32))
             return words
 
-        offs_t = load_list(offs, "offs_t")
         tab_sc = kept([P, T], U8, "tab_sc")
         wox_sc = kept([P, R_PASSES, N], U8, "wox_sc")
         nc.vector.memset(tab_sc[:].bitcast(I32), 0)
@@ -74,6 +74,7 @@ def tile_list_sherd_vessel_joining_kernel(
 
         raw, tab_w = {}, {}
         tab_w[0] = load_table(0, 0)
+        offs_t = load_list(offs, "offs_t")
         for q in range(QUADRANTS):
             nc.sync.dma_start(
                 tab_sc[32 * q : 32 * q + 4 * K_PASSES, :].bitcast(I32),
@@ -219,7 +220,7 @@ def tile_list_sherd_vessel_joining_kernel(
         round_late(2, 1)
 
         prod = [placed([P, PACK, M], F32, "prod%d" % b, (56, 80)[b]) for b in range(R_PASSES)]
-        damp = [placed([P, PACK, M], F32, "damp%d" % b, (48, 64)[b]) for b in range(R_PASSES)]
+        damp = [placed([P, PACK, M], F32, "damp0", 48)]
         body, z_rounded, z_q = {}, {}, {}
 
         def pick_body(g, m0, width, dst):
@@ -269,22 +270,27 @@ def tile_list_sherd_vessel_joining_kernel(
         roots = placed([P, 2, M], F32, "roots", 94)
         inverse_root(roots[:], damp[0][:, 2:PACK, :])
         h_out(6)
-        h_out(7)
         square(damp[0][:, 2:PACK, :], roots[:])
-        wrd0_rounded = placed([P, PACK * N], BF16, "wrd0_rounded", 34)
-        scalar_round(wrd0_rounded[:], wrd_raw[0][:])
+        h_out(7)
         wrd1_rounded = placed([P, PACK * PASS], BF16, "wrd1_rounded", 40)
 
-        for g in range(PACK, PACK + 2):
-            pick_all(g, body_buffer(), damp[1][:, g - PACK, :])
+        for g, dst in ((4, body_buffer()), (5, placed([P, M], F32, "body5", 117)[:])):
+            pick_body(g, 0, M, dst)
+            pick_base(g, 0, M)
+        damp.append(placed([P, PACK, M], F32, "damp1", 118))
+        for g in (4, 5):
+            pick_rim(g, damp[1][:, g - PACK, :])
+        wrd0_rounded = placed([P, PACK * N], BF16, "wrd0_rounded", 112)
+        gpsimd_round(wrd0_rounded[:, 0 : PACK * SHARE], wrd_raw[0][:, :, 0:SHARE])
+        scalar_round(wrd0_rounded[:, PACK * SHARE : PACK * N], wrd_raw[0][:, :, SHARE:N])
         z_rounded[(0, 0)] = placed([P, PACK * M], BF16, "z_rounded0", 100)
         round_z(0, 0, M_HALF, z_rounded[(0, 0)][:, 0 : PACK * M_HALF])
         pick_body(6, 0, M, placed([P, M], F32, "body6", 92.5)[:])
         round_z(0, M_HALF, M_HALF, z_rounded[(0, 0)][:, PACK * M_HALF : PACK * M])
         pick_base(6, 0, M)
-        rims = [placed([P, M], F32, "rim%d" % (6 + u), 94.5 + 2 * u) for u in range(2)]
+        last_rims = placed([P, 2, M], F32, "last_rims", 95)
         for u in range(2):
-            pick_rim(6 + u, rims[u][:])
+            pick_rim(6 + u, last_rims[:, u, :])
         wrd1_front = placed([P, PACK * (N - PASS)], BF16, "wrd1_front", 92.5)
         gpsimd_round(wrd1_front[:], wrd_raw[1][:, :, 0 : N - PASS])
         x = damp[1][:, 0:2, :]
@@ -295,11 +301,12 @@ def tile_list_sherd_vessel_joining_kernel(
         square(x, x)
         halves = [damp[1][:, 2:PACK, m0 : m0 + M_HALF] for m0 in (0, M_HALF)]
         half_roots = placed([P, 2, M_HALF], F32, "half_roots", 108)
-        for u in range(2):
-            square(damp[1][:, 2 + u, :], rims[u][:])
+        square(halves[0], last_rims[:, :, 0:M_HALF])
         inverse_root(half_roots[:], halves[0])
-        inverse_root(halves[1], halves[1])
         square(halves[0], half_roots[:])
+        half_squares = placed([P, 2, M_HALF], F32, "half_squares", 109)
+        square(half_squares[:], last_rims[:, :, M_HALF:M])
+        inverse_root(halves[1], half_squares[:])
         square(halves[1], halves[1])
 
         wrd_q = [[], []]
@@ -342,14 +349,18 @@ def tile_list_sherd_vessel_joining_kernel(
                     stop=(b == R_PASSES - 1 and u == 1),
                 )
 
-        def y_out(m0, pair):
+        def y_out(m0, pair, pieces=1):
             res = placed([P, BANK], F32, "res_%d_%d" % (m0, pair), 8 + 2 * (PAIRS * (m0 // M_HALF) + pair))
             nc.scalar.copy(res[:], y_ps[(m0, pair, OX)][:])
-            nc.vector.tensor_tensor(res[:], y_ps[(m0, pair, RD)][:], res[:], MAX)
-            nc.sync.dma_start(
-                out[2 * pair * P : (2 * pair + 2) * P, m0 : m0 + M_HALF].rearrange("(u p) m -> p u m", u=2),
-                res[:].rearrange("p (u m) -> p u m", u=2),
-            )
+            tiles = 2 // pieces
+            for u0 in range(0, 2, tiles):
+                cols = slice(u0 * M_HALF, (u0 + tiles) * M_HALF)
+                rows = slice((2 * pair + u0) * P, (2 * pair + u0 + tiles) * P)
+                nc.vector.tensor_tensor(res[:, cols], y_ps[(m0, pair, RD)][:, cols], res[:, cols], MAX)
+                nc.sync.dma_start(
+                    out[rows, m0 : m0 + M_HALF].rearrange("(u p) m -> p u m", u=tiles),
+                    res[:, cols].rearrange("p (u m) -> p u m", u=tiles),
+                )
 
         first_banks = [(0, pair, style) for style in (OX, RD) for pair in range(PAIRS)]
         second_banks = [(M_HALF, pair, style) for pair in range(PAIRS) for style in (OX, RD)]
@@ -383,4 +394,4 @@ def tile_list_sherd_vessel_joining_kernel(
                 y_pass(0, M_HALF, pair, style)
             y_pass(1, M_HALF, pair, style)
         for pair in range(PAIRS):
-            y_out(M_HALF, pair)
+            y_out(M_HALF, pair, 2 if pair == PAIRS - 1 else 1)

@@ -31,7 +31,6 @@ M_HALF = M // 2
 PAIRS = N // (2 * P)
 RIM, BODY, BASE = 0, 1, 2
 OX, RD = 0, 1
-SHARE = 224
 LAST = PACK - 1
 
 
@@ -260,63 +259,58 @@ def tile_list_sherd_vessel_joining_kernel(
             quantize_late(u)
             rims.append(placed([P, M], F32, "rim%d" % (2 + u), 74 + 16 * u))
             pick_all(2 + u, placed([P, M], F32, "body%d" % (2 + u), 72 + 16 * u)[:], rims[u][:])
-        square(damp[0][:, 0:2, :], damp[0][:, 0:2, :])
+        early, later = damp[0][:, 0:2, :], damp[0][:, 2:PACK, :]
+        square(early, early)
         h_out(4)
         h_out(5)
-        inverse_root(damp[0][:, 0:2, :], damp[0][:, 0:2, :])
+        inverse_root(early, early)
         for u in range(2):
             square(damp[0][:, 2 + u, :], rims[u][:])
-        square(damp[0][:, 0:2, :], damp[0][:, 0:2, :])
-        roots = placed([P, 2, M], F32, "roots", 94)
-        inverse_root(roots[:], damp[0][:, 2:PACK, :])
         h_out(6)
-        square(damp[0][:, 2:PACK, :], roots[:])
+        square(early, early)
+        inverse_root(later, later)
         h_out(7)
-        wrd1_rounded = placed([P, PACK * PASS], BF16, "wrd1_rounded", 40)
+        square(later, later)
 
-        for g, dst in ((4, body_buffer()), (5, placed([P, M], F32, "body5", 117)[:])):
+        wrd0_back = placed([P, PACK * (N - PASS)], BF16, "wrd0_back", 40)
+        scalar_round(wrd0_back[:], wrd_raw[0][:, :, PASS:N])
+        wrd1_rounded = placed([P, PACK * N], BF16, "wrd1_rounded", 34)
+        scalar_round(wrd1_rounded[:], wrd_raw[1][:])
+
+        for g, dst in ((4, body_buffer()), (5, body_buffer()), (6, placed([P, M], F32, "body6", 117)[:])):
             pick_body(g, 0, M, dst)
             pick_base(g, 0, M)
-        damp.append(placed([P, PACK, M], F32, "damp1", 118))
-        for g in (4, 5):
-            pick_rim(g, damp[1][:, g - PACK, :])
-        wrd0_rounded = placed([P, PACK * N], BF16, "wrd0_rounded", 112)
-        gpsimd_round(wrd0_rounded[:, 0 : PACK * SHARE], wrd_raw[0][:, :, 0:SHARE])
-        scalar_round(wrd0_rounded[:, PACK * SHARE : PACK * N], wrd_raw[0][:, :, SHARE:N])
-        z_rounded[(0, 0)] = placed([P, PACK * M], BF16, "z_rounded0", 100)
-        round_z(0, 0, M_HALF, z_rounded[(0, 0)][:, 0 : PACK * M_HALF])
-        pick_body(6, 0, M, placed([P, M], F32, "body6", 92.5)[:])
-        round_z(0, M_HALF, M_HALF, z_rounded[(0, 0)][:, PACK * M_HALF : PACK * M])
-        pick_base(6, 0, M)
-        last_rims = placed([P, 2, M], F32, "last_rims", 95)
-        for u in range(2):
-            pick_rim(6 + u, last_rims[:, u, :])
-        wrd1_front = placed([P, PACK * (N - PASS)], BF16, "wrd1_front", 92.5)
-        gpsimd_round(wrd1_front[:], wrd_raw[1][:, :, 0 : N - PASS])
+        late_rims = placed([P, PACK, M], F32, "late_rims", 118)
+        for t in range(PACK):
+            pick_rim(PACK + t, late_rims[:, t, :])
+        wrd0_front = placed([P, PACK * PASS], BF16, "wrd0_front", 114)
+        gpsimd_round(wrd0_front[:], wrd_raw[0][:, :, 0:PASS])
+        damp.append(placed([P, PACK, M], F32, "damp1", 64))
         x = damp[1][:, 0:2, :]
-        square(x, x)
-        scalar_round(wrd1_rounded[:, 0 : 2 * PACK * P], wrd_raw[1][:, :, 2 * P : 4 * P])
-        inverse_root(x, x)
-        scalar_round(wrd1_rounded[:, 2 * PACK * P : 4 * PACK * P], wrd_raw[1][:, :, 4 * P : N])
-        square(x, x)
+        square(x, late_rims[:, 0:2, :])
         halves = [damp[1][:, 2:PACK, m0 : m0 + M_HALF] for m0 in (0, M_HALF)]
         half_roots = placed([P, 2, M_HALF], F32, "half_roots", 108)
-        square(halves[0], last_rims[:, :, 0:M_HALF])
+        inverse_root(x, x)
+        square(halves[0], late_rims[:, 2:PACK, 0:M_HALF])
+        square(x, x)
         inverse_root(half_roots[:], halves[0])
         square(halves[0], half_roots[:])
         half_squares = placed([P, 2, M_HALF], F32, "half_squares", 109)
-        square(half_squares[:], last_rims[:, :, M_HALF:M])
+        square(half_squares[:], late_rims[:, 2:PACK, M_HALF:M])
         inverse_root(halves[1], half_squares[:])
         square(halves[1], halves[1])
 
+        z_rounded[(0, 0)] = placed([P, PACK * M], BF16, "z_rounded0", 7)
+        round_z(0, 0, M, z_rounded[(0, 0)][:])
         wrd_q = [[], []]
-        wrd_q[0].extend(blocks(quantize("wrd_0a", wrd0_rounded[:, 0 : PACK * PASS])))
-        wrd_q[0].extend(blocks(quantize("wrd_0b", wrd0_rounded[:, PACK * PASS : PACK * N])))
-        quantize_z(0, 0, placed([P, M], U32, "z0_codes", 20))
-        pick_body(7, 0, M_HALF, placed([P, M_HALF], F32, "last_body", 22)[:])
-        wrd_q[1].extend(blocks(quantize("wrd_1a", wrd1_front[:])))
+        wrd_q[0].extend(blocks(quantize("wrd_0a", wrd0_front[:])))
+        quantize_z(0, 0)
+        wrd_q[0].extend(blocks(quantize("wrd_0b", wrd0_back[:], placed([P, N - PASS], U32, "wrd_0b_codes", 15))))
+        pick_body(7, 0, M_HALF, placed([P, M_HALF], F32, "last_body", 11)[:])
+        late_codes = [placed([P, PASS], U32, "wrd_1a_codes", 12), placed([P, N - PASS], U32, "wrd_1b_codes", 14)]
+        wrd_q[1].extend(blocks(quantize("wrd_1a", wrd1_rounded[:, 0 : PACK * PASS], late_codes[0])))
         pick_base(7, 0, M_HALF)
-        wrd_q[1].extend(blocks(quantize("wrd_1b", wrd1_rounded[:])))
+        wrd_q[1].extend(blocks(quantize("wrd_1b", wrd1_rounded[:, PACK * PASS : PACK * N], late_codes[1])))
 
         y_ps = {}
 
@@ -350,7 +344,7 @@ def tile_list_sherd_vessel_joining_kernel(
                 )
 
         def y_out(m0, pair, pieces=1):
-            res = placed([P, BANK], F32, "res_%d_%d" % (m0, pair), 8 + 2 * (PAIRS * (m0 // M_HALF) + pair))
+            res = placed([P, BANK], F32, "res_%d_%d" % (m0, pair), 20 + 2 * (PAIRS * (m0 // M_HALF) + pair))
             nc.scalar.copy(res[:], y_ps[(m0, pair, OX)][:])
             tiles = 2 // pieces
             for u0 in range(0, 2, tiles):

@@ -15,7 +15,6 @@ FP8X4 = mybir.dt.float8_e4m3fn_x4
 FP4X4 = mybir.dt.float4_e2m1fn_x4
 ACT = mybir.ActivationFunctionType
 MULT = mybir.AluOpType.mult
-ADD = mybir.AluOpType.add
 MAX = mybir.AluOpType.max
 
 P = 128
@@ -27,11 +26,11 @@ QUADRANTS = 4
 LIST_GROUP = 16
 BANK = 512
 LINE = 4
-M_HALF = M // 2
-PAIRS = N // (2 * P)
+HALF = M // 2
+QUARTER = M // 4
+N_TILES = N // P
 RIM, BODY, BASE = 0, 1, 2
 OX, RD = 0, 1
-LAST = PACK - 1
 
 
 def tile_list_sherd_vessel_joining_kernel(
@@ -40,7 +39,7 @@ def tile_list_sherd_vessel_joining_kernel(
     nc = tc.nc
     with ExitStack() as ctx:
         keep = ctx.enter_context(tc.tile_pool(name="keep", bufs=1))
-        ring = ctx.enter_context(tc.tile_pool(name="ring", bufs=PACK + 1))
+        ring = ctx.enter_context(tc.tile_pool(name="ring", bufs=4))
         shared = ctx.enter_context(tc.tile_pool(name="shared", bufs=1))
         psum = ctx.enter_context(tc.psum_pool(name="psum", bufs=8))
 
@@ -93,23 +92,14 @@ def tile_list_sherd_vessel_joining_kernel(
         )
         warm = keep.tile([P, 1], F32, name="warm")
         nc.scalar.activation(warm[:], gain_t[:, 0:1], ACT.Abs_reciprocal_sqrt, bias=1.0, scale=0.0)
-        gain_rows = kept([P, R_PASSES * PACK, M], F32, "gain_rows")
-        for b in range(R_PASSES):
-            some = slice(b * PACK, (b + 1) * PACK)
-            nc.scalar.activation(gain_rows[:, some, :], gain_t[:, some].unsqueeze(2).to_broadcast([P, PACK, M]), ACT.Copy)
 
         v_w = [kept([P, S], U32, "v_w%d" % a) for a in range(K_PASSES)]
         v_sc = kept([P, S], U8, "v_sc")
 
-        def gather_words(a, j0, width):
-            entries = offs_t[:, j0 // LIST_GROUP : (j0 + width) // LIST_GROUP]
-            nc.vector.tensor_copy(v_w[a][:, j0 : j0 + width], tab_w[a][:].indirect(entries))
-
-        def quantize(name, rounded, codes=None):
+        def quantize(name, rounded):
             width = rounded.shape[1] // PACK
             scales = kept([P, width], U8, name + "_scales")
-            if codes is None:
-                codes = kept([P, width], U32, name + "_codes")
+            codes = kept([P, width], U32, name + "_codes")
             nc.vector.quantize_mx(out=codes[:].bitcast(FP8X4), scales=scales[:], in_=rounded)
             return codes, scales
 
@@ -117,26 +107,15 @@ def tile_list_sherd_vessel_joining_kernel(
             codes, scales = pair
             return [(codes[:, c : c + P], scales[:, c : c + P]) for c in range(0, codes.shape[1], P)]
 
-        def scalar_round(dst, src):
-            nc.scalar.copy(
-                dst.rearrange("p (c i j) -> p c j i", i=LINE, j=PACK), src.rearrange("p j (c i) -> p c j i", i=LINE)
-            )
-
-        def gpsimd_round(dst, src):
-            nc.gpsimd.tensor_scalar(
-                dst.rearrange("p (c j) -> p c j", j=PACK), src.rearrange("p j c -> p c j"), 1.0, 0.0, MULT, ADD
-            )
-
-        def round_w1(b, a, u, dst, copy=nc.scalar.copy):
+        def round_w1(b, a, u, dst, copy):
             src = raw[(b, a)][:].rearrange("p j (m t) -> p m j t", t=PACK)
             copy(dst.rearrange("p (s m j) -> p m j s", s=2, j=PACK), src[:, :, :, 2 * u : 2 * u + 2])
 
         w1_q, h_ps, h_sb = {}, {}, {}
 
-        def quantize_w1(name, rounded, passes, tiles, codes=None):
-            made = blocks(quantize(name, rounded, codes))
-            for n, key in enumerate([(g, a) for a in passes for g in tiles]):
-                w1_q[key] = made[n]
+        def quantize_w1(name, rounded, a, tiles):
+            for g, block in zip(tiles, blocks(quantize(name, rounded))):
+                w1_q[(g, a)] = block
 
         def h_pass(g, bank, a):
             if a == 0:
@@ -153,40 +132,29 @@ def tile_list_sherd_vessel_joining_kernel(
                 stop=(a == K_PASSES - 1),
             )
 
-        def h_product(tiles):
-            for g in tiles:
-                for bank in range(S // BANK):
-                    for a in range(K_PASSES):
-                        h_pass(g, bank, a)
-
-        def h_out(g, tile=None, second_copy=nc.scalar.copy):
-            h_sb[g] = ring.tile([P, S], F32, name="h", tag="h", align_bytes=64) if tile is None else tile
-            nc.scalar.copy(h_sb[g][:, 0:BANK], h_ps[(g, 0)][:])
-            second_copy(h_sb[g][:, BANK:S], h_ps[(g, 1)][:])
+        def h_out(g, bank):
+            if bank == 0:
+                h_sb[g] = kept([P, S], F32, "h%d" % g)
+            nc.scalar.copy(h_sb[g][:, bank * BANK : (bank + 1) * BANK], h_ps[(g, bank)][:])
 
         def picked(g, which, m0, width):
             return h_sb[g][:].indirect(pos_t[which][:, m0 // LIST_GROUP : (m0 + width) // LIST_GROUP])
 
-        def square(dst, src):
-            nc.scalar.activation(dst, src, ACT.Square)
-
-        def inverse_root(dst, src):
-            nc.scalar.activation(dst, src, ACT.Abs_reciprocal_sqrt, bias=1.0)
-
+        def scalar_pick(dst, src):
+            nc.scalar.activation(dst, src, ACT.Copy)
 
         for a in range(K_PASSES):
-            gather_words(a, 0, S)
+            nc.vector.tensor_copy(v_w[a][:], tab_w[a][:].indirect(offs_t[:]))
             if a == 0:
                 nc.vector.tensor_copy(v_sc[:], tab_sc[:].indirect(offs_t[:]))
             for u in range(2):
-                rounded = ring.tile([P, 2 * PACK * P], BF16, name="narrow", tag="narrow", bufs=4, align_bytes=64)
+                rounded = ring.tile([P, 2 * PACK * P], BF16, name="narrow", tag="narrow", align_bytes=64)
                 round_w1(0, a, u, rounded[:], (nc.vector.tensor_copy, nc.scalar.copy)[u])
-                codes = placed([P, 2 * P], U32, "first_codes%d" % u, 33.5 + 6 * u) if a == K_PASSES - 1 else None
-                quantize_w1("w1_0%d%d" % (a, u), rounded[:], [a], [2 * u, 2 * u + 1], codes)
+                quantize_w1("w1_0%d%d" % (a, u), rounded[:], a, [2 * u, 2 * u + 1])
             for g in range(PACK):
                 for bank in range(S // BANK):
                     h_pass(g, bank, a)
-        wrd_raw = [load_rows(wrd, "wrd_raw%d" % b, b, 0, N, 8 + 12 * b) for b in range(R_PASSES)]
+        wrd_raw = [load_rows(wrd, "wrd_raw%d" % b, b, 0, N, 32 * b) for b in range(R_PASSES)]
         wox_w = kept([P, R_PASSES, 2 * N], U8, "wox_w")
         nc.sync.dma_start(wox_w[:].bitcast(I32), wox_words.rearrange("b p c -> p b c").bitcast(I32))
         for q in range(QUADRANTS):
@@ -195,197 +163,251 @@ def tile_list_sherd_vessel_joining_kernel(
                 wox_scales[:, 4 * q : 4 * q + 4, :].rearrange("b r n -> r b n").bitcast(I32),
             )
 
-        late_first = [placed([P, 2, 2 * PACK * P], BF16, "late_first%d" % u, 34 + 6 * u) for u in range(2)]
-        late_last = [placed([P, 2 * PACK * P], BF16, "late_last%d" % u, 38 + 6 * u) for u in range(2)]
+        late = [kept([P, PACK * PASS], BF16, "late%d" % a) for a in range(K_PASSES)]
 
-        def round_late(a, u):
-            round_w1(1, a, u, late_first[u][:, a, :] if a < 2 else late_last[u][:])
+        def round_late(a):
+            for u in range(2):
+                round_w1(1, a, u, late[a][:, 2 * u * PASS : 2 * (u + 1) * PASS], nc.vector.tensor_copy)
 
-        def quantize_late(u):
-            tiles = [PACK + 2 * u, PACK + 2 * u + 1]
-            quantize_w1("late_first%d" % u, late_first[u][:].rearrange("p a c -> p (a c)"), [0, 1], tiles)
-            quantize_w1("late_last%d" % u, late_last[u][:], [2], tiles)
-            h_product(tiles)
+        def quantize_late(a):
+            quantize_w1("late%d" % a, late[a][:], a, range(PACK, 2 * PACK))
 
-        h_out(0, second_copy=nc.vector.tensor_copy)
-        h_out(1)
-        round_late(0, 0)
-        round_late(1, 0)
-        h_out(2)
-        round_late(2, 0)
-        round_late(0, 1)
-        h_out(3)
-        round_late(1, 1)
-        round_late(2, 1)
+        wrd_rounded, wrd_q = {}, {}
 
-        prod = [placed([P, PACK, M], F32, "prod%d" % b, (56, 80)[b]) for b in range(R_PASSES)]
-        damp = [placed([P, PACK, M], F32, "damp0", 48)]
+        def round_wrd(b):
+            wrd_rounded[b] = placed([P, PACK * N], BF16, "wrd_rounded%d" % b, (88, 56)[b])
+            nc.vector.tensor_copy(
+                wrd_rounded[b][:].rearrange("p (c i j) -> p c j i", i=LINE, j=PACK),
+                wrd_raw[b][:].rearrange("p j (c i) -> p c j i", i=LINE),
+            )
+
+        def quantize_wrd(b):
+            half = PACK * N // 2
+            wrd_q[b] = [
+                block
+                for c in (0, half)
+                for block in blocks(quantize("wrd_%d_%d" % (b, c), wrd_rounded[b][:, c : c + half]))
+            ]
+
+        damp = {
+            (0, 0): placed([P, PACK, M], F32, "damp0", 56),
+            (1, 0): placed([P, PACK, HALF], F32, "damp1a", 72),
+            (1, HALF): placed([P, PACK, HALF], F32, "damp1b", 76),
+        }
+        prod = {
+            (0, 0): placed([P, PACK, M], F32, "prod0", 48),
+            (1, 0): placed([P, PACK, HALF], F32, "prod1a", 64),
+            (1, HALF): placed([P, PACK, QUARTER], F32, "prod1b", 68),
+            (1, HALF + QUARTER): placed([P, PACK, QUARTER], F32, "prod1c", 70),
+        }
         body, z_rounded, z_q = {}, {}, {}
 
-        def pick_body(g, m0, width, dst):
-            nc.vector.tensor_tensor(dst, picked(g, BODY, m0, width), gain_rows[:, g, 0:width], MULT)
-            body[(g, m0)] = dst
+        def pick_body(g, m0, width, pick=scalar_pick):
+            body[(g, m0)] = kept([P, width], F32, "body%d_%d" % (g, m0))
+            pick(body[(g, m0)][:], picked(g, BODY, m0, width))
 
-        def pick_rim(g, dst):
-            nc.vector.tensor_copy(dst, picked(g, RIM, 0, M))
+        def pick_rim(g, m0, pick=scalar_pick):
+            dst = damp[(g // PACK, m0)][:, g % PACK, :]
+            pick(dst, picked(g, RIM, m0, dst.shape[1]))
 
-        def pick_base(g, m0, width):
-            dst = prod[g // PACK][:, g % PACK, m0 : m0 + width]
-            nc.vector.tensor_tensor(dst, picked(g, BASE, m0, width), body[(g, m0)], MULT)
+        def pick_base(g, m0):
+            dst = prod[(g // PACK, m0)][:, g % PACK, :]
+            nc.vector.tensor_tensor(dst, picked(g, BASE, m0, dst.shape[1]), body[(g, m0)][:], MULT)
 
-        def pick_all(g, body_dst, rim_dst):
-            pick_body(g, 0, M, body_dst)
-            pick_rim(g, rim_dst)
-            pick_base(g, 0, M)
+        def square(x):
+            nc.scalar.activation(x, x, ACT.Square)
 
-        def body_buffer():
-            return ring.tile([P, M], F32, name="body", tag="body", bufs=2, align_bytes=64)[:]
+        def inverse_root(x):
+            nc.scalar.activation(x, x, ACT.Abs_reciprocal_sqrt, bias=1.0)
 
-        def round_z(b, m0, width, rounded):
+        def gained_square(g, m0):
+            x = damp[(g // PACK, m0)][:, g % PACK, :]
+            nc.vector.scalar_tensor_tensor(x, x, gain_t[:, g : g + 1], x, MULT, MULT)
+
+        def round_z(b, m0, damping, kib):
+            width = prod[(b, m0)].shape[2]
+            z_rounded[(b, m0)] = placed([P, PACK * width], BF16, "z_rounded%d_%d" % (b, m0), kib)
             nc.vector.tensor_tensor(
-                rounded.rearrange("p (c i t) -> p c t i", i=LINE, t=PACK),
-                prod[b][:, :, m0 : m0 + width].rearrange("p t (c i) -> p c t i", i=LINE),
-                damp[b][:, :, m0 : m0 + width].rearrange("p t (c i) -> p c t i", i=LINE),
+                z_rounded[(b, m0)][:].rearrange("p (c i t) -> p c t i", i=LINE, t=PACK),
+                prod[(b, m0)][:].rearrange("p t (c i) -> p c t i", i=LINE),
+                damping.rearrange("p t (c i) -> p c t i", i=LINE),
                 MULT,
             )
 
-        def quantize_z(b, m0, codes=None):
-            z_q[(b, m0)] = quantize("z_%d_%d" % (b, m0), z_rounded[(b, m0)][:], codes)
+        def quantize_z(b, m0):
+            z_q[(b, m0)] = quantize("z_%d_%d" % (b, m0), z_rounded[(b, m0)][:])
 
-        for g in range(2):
-            pick_all(g, body_buffer(), damp[0][:, g, :])
-        rims = []
-        for u in range(2):
-            quantize_late(u)
-            rims.append(placed([P, M], F32, "rim%d" % (2 + u), 74 + 16 * u))
-            pick_all(2 + u, placed([P, M], F32, "body%d" % (2 + u), 72 + 16 * u)[:], rims[u][:])
-        early, later = damp[0][:, 0:2, :], damp[0][:, 2:PACK, :]
-        square(early, early)
-        h_out(4)
-        h_out(5)
-        inverse_root(early, early)
-        for u in range(2):
-            square(damp[0][:, 2 + u, :], rims[u][:])
-        h_out(6)
-        square(early, early)
-        inverse_root(later, later)
-        h_out(7)
-        square(later, later)
+        h_out(0, 0)
+        h_out(0, 1)
+        h_out(1, 0)
+        pick_body(0, 0, M)
+        round_late(0)
+        pick_rim(0, 0, nc.vector.tensor_copy)
+        quantize_late(0)
+        h_out(1, 1)
+        h_out(2, 0)
+        pick_base(0, 0)
+        round_late(1)
+        pick_body(1, 0, M)
+        pick_rim(1, 0)
+        pick_base(1, 0)
+        quantize_late(1)
+        h_out(2, 1)
+        round_late(2)
+        h_out(3, 0)
+        pick_body(2, 0, M)
+        pick_rim(2, 0, nc.vector.tensor_copy)
+        quantize_late(2)
+        for g in range(PACK, 2 * PACK):
+            for bank in range(S // BANK):
+                for a in range(K_PASSES):
+                    h_pass(g, bank, a)
+        h_out(3, 1)
+        square(damp[(0, 0)][:, 0:2, :])
+        pick_base(2, 0)
+        pick_rim(3, 0)
+        inverse_root(damp[(0, 0)][:, 0:2, :])
+        pick_body(3, 0, M)
+        square(damp[(0, 0)][:, 2:PACK, :])
+        round_wrd(0)
+        h_out(4, 0)
+        pick_base(3, 0)
+        inverse_root(damp[(0, 0)][:, 2:PACK, :])
+        gained_square(0, 0)
+        gained_square(1, 0)
+        quantize_wrd(0)
+        gained_square(2, 0)
+        gained_square(3, 0)
+        round_z(0, 0, damp[(0, 0)][:], 80)
 
-        wrd0_back = placed([P, PACK * (N - PASS)], BF16, "wrd0_back", 40)
-        scalar_round(wrd0_back[:], wrd_raw[0][:, :, PASS:N])
-        wrd1_rounded = placed([P, PACK * N], BF16, "wrd1_rounded", 34)
-        scalar_round(wrd1_rounded[:], wrd_raw[1][:])
-
-        for g, dst in ((4, body_buffer()), (5, body_buffer()), (6, placed([P, M], F32, "body6", 117)[:])):
-            pick_body(g, 0, M, dst)
-            pick_base(g, 0, M)
-        late_rims = placed([P, PACK, M], F32, "late_rims", 118)
-        for t in range(PACK):
-            pick_rim(PACK + t, late_rims[:, t, :])
-        wrd0_front = placed([P, PACK * PASS], BF16, "wrd0_front", 114)
-        gpsimd_round(wrd0_front[:], wrd_raw[0][:, :, 0:PASS])
-        damp.append(placed([P, PACK, M], F32, "damp1", 64))
-        x = damp[1][:, 0:2, :]
-        square(x, late_rims[:, 0:2, :])
-        halves = [damp[1][:, 2:PACK, m0 : m0 + M_HALF] for m0 in (0, M_HALF)]
-        half_roots = placed([P, 2, M_HALF], F32, "half_roots", 108)
-        inverse_root(x, x)
-        square(halves[0], late_rims[:, 2:PACK, 0:M_HALF])
-        square(x, x)
-        inverse_root(half_roots[:], halves[0])
-        square(halves[0], half_roots[:])
-        half_squares = placed([P, 2, M_HALF], F32, "half_squares", 109)
-        square(half_squares[:], late_rims[:, 2:PACK, M_HALF:M])
-        inverse_root(halves[1], half_squares[:])
-        square(halves[1], halves[1])
-
-        z_rounded[(0, 0)] = placed([P, PACK * M], BF16, "z_rounded0", 7)
-        round_z(0, 0, M, z_rounded[(0, 0)][:])
-        wrd_q = [[], []]
-        wrd_q[0].extend(blocks(quantize("wrd_0a", wrd0_front[:])))
+        late_tiles = range(PACK, 2 * PACK)
+        h_out(4, 1)
+        for g in late_tiles[:-1]:
+            h_out(g + 1, 0)
+            pick_rim(g, 0)
+            h_out(g + 1, 1)
+            pick_body(g, 0, HALF)
+        pick_rim(7, 0)
+        pick_body(7, 0, HALF)
+        pick_base(4, 0)
         quantize_z(0, 0)
-        wrd_q[0].extend(blocks(quantize("wrd_0b", wrd0_back[:], placed([P, N - PASS], U32, "wrd_0b_codes", 15))))
-        pick_body(7, 0, M_HALF, placed([P, M_HALF], F32, "last_body", 11)[:])
-        late_codes = [placed([P, PASS], U32, "wrd_1a_codes", 12), placed([P, N - PASS], U32, "wrd_1b_codes", 14)]
-        wrd_q[1].extend(blocks(quantize("wrd_1a", wrd1_rounded[:, 0 : PACK * PASS], late_codes[0])))
-        pick_base(7, 0, M_HALF)
-        wrd_q[1].extend(blocks(quantize("wrd_1b", wrd1_rounded[:, PACK * PASS : PACK * N], late_codes[1])))
+        pick_base(5, 0)
+        round_wrd(1)
+        pick_base(6, 0)
+        pick_base(7, 0)
+        quantize_wrd(1)
+        square(damp[(1, 0)][:])
+        pick_rim(4, HALF)
+        inverse_root(damp[(1, 0)][:])
 
         y_ps = {}
 
-        def y_pass(b, m0, pair, style):
-            z_codes, z_scales = z_q[(0, 0)] if b == 0 else z_q[(1, m0)]
-            z0 = m0 if b == 0 else 0
-            steps = M_HALF // P
-            for u in range(2 if style == OX else 0):
-                n0 = (2 * pair + u) * P
-                for s in range(steps):
-                    cols = slice(z0 + s * P, z0 + (s + 1) * P)
-                    nc.tensor.matmul_mx(
-                        out=y_ps[(m0, pair, OX)][:, u * M_HALF + s * P : u * M_HALF + (s + 1) * P],
-                        lhsT=wox_w[:, b, 2 * n0 : 2 * (n0 + P)].bitcast(FP4X4),
-                        lhsT_scale=wox_sc[:, b, n0 : n0 + P],
-                        rhs=z_codes[:, cols].bitcast(FP8X4),
-                        rhs_scale=z_scales[:, cols],
-                        start=(b == 0 and u == 0 and s == 0),
-                        stop=(b == R_PASSES - 1 and u == 1 and s == steps - 1),
-                    )
-            for u in range(2 if style == RD else 0):
-                codes, scales = wrd_q[b][2 * pair + u]
+        def open_bank(m0, width, sums):
+            y_ps[(m0, sums)] = psum.tile([P, len(sums), width], F32, name="bank", tag="bank")
+
+        def y_pass(b, m0, sums):
+            bank = y_ps[(m0, sums)]
+            width = bank.shape[2]
+            z_codes, z_scales = z_q[(b, m0 * b)]
+            cols = slice(m0 * (1 - b), m0 * (1 - b) + width)
+            for u, (style, n) in enumerate(sums):
+                if style == OX:
+                    codes, scales = wox_w[:, b, 2 * n * P : 2 * (n + 1) * P].bitcast(FP4X4), wox_sc[:, b, n * P : (n + 1) * P]
+                else:
+                    codes, scales = wrd_q[b][n][0].bitcast(FP8X4), wrd_q[b][n][1]
                 nc.tensor.matmul_mx(
-                    out=y_ps[(m0, pair, RD)][:, u * M_HALF : (u + 1) * M_HALF],
-                    lhsT=codes.bitcast(FP8X4),
+                    out=bank[:, u, :],
+                    lhsT=codes,
                     lhsT_scale=scales,
-                    rhs=z_codes[:, z0 : z0 + M_HALF].bitcast(FP8X4),
-                    rhs_scale=z_scales[:, z0 : z0 + M_HALF],
+                    rhs=z_codes[:, cols].bitcast(FP8X4),
+                    rhs_scale=z_scales[:, cols],
                     start=(b == 0 and u == 0),
-                    stop=(b == R_PASSES - 1 and u == 1),
+                    stop=(b == R_PASSES - 1 and u == len(sums) - 1),
                 )
 
-        def y_out(m0, pair, pieces=1):
-            res = placed([P, BANK], F32, "res_%d_%d" % (m0, pair), 20 + 2 * (PAIRS * (m0 // M_HALF) + pair))
-            nc.scalar.copy(res[:], y_ps[(m0, pair, OX)][:])
-            tiles = 2 // pieces
-            for u0 in range(0, 2, tiles):
-                cols = slice(u0 * M_HALF, (u0 + tiles) * M_HALF)
-                rows = slice((2 * pair + u0) * P, (2 * pair + u0 + tiles) * P)
-                nc.vector.tensor_tensor(res[:, cols], y_ps[(m0, pair, RD)][:, cols], res[:, cols], MAX)
-                nc.sync.dma_start(
-                    out[rows, m0 : m0 + M_HALF].rearrange("(u p) m -> p u m", u=tiles),
-                    res[:, cols].rearrange("p (u m) -> p u m", u=tiles),
-                )
+        res = {}
 
-        first_banks = [(0, pair, style) for style in (OX, RD) for pair in range(PAIRS)]
-        second_banks = [(M_HALF, pair, style) for pair in range(PAIRS) for style in (OX, RD)]
-        for key in first_banks + second_banks:
-            y_ps[key] = psum.tile([P, BANK], F32, name="bank", tag="bank")
-        for pair in range(PAIRS):
-            y_pass(0, 0, pair, OX)
-        y_pass(0, M_HALF, 0, OX)
-        for pair in range(PAIRS):
-            y_pass(0, 0, pair, RD)
-        y_pass(0, M_HALF, 0, RD)
+        def y_copy(m0, ox_sums, kib):
+            bank = y_ps[(m0, ox_sums)]
+            count = len([style for style, n in ox_sums if style == OX])
+            res[(m0, ox_sums)] = placed([P, count, bank.shape[2]], F32, "res_%d_%d" % (m0, ox_sums[0][1]), kib)
+            nc.scalar.copy(res[(m0, ox_sums)][:], bank[:, 0:count, :])
 
-        for m0 in (0, M_HALF):
-            z_rounded[(1, m0)] = placed([P, PACK * M_HALF], BF16, "z_rounded1_%d" % m0, 104 + 2 * (m0 // M_HALF))
-        round_z(1, 0, M_HALF, z_rounded[(1, 0)][:])
-        pick_body(7, M_HALF, M_HALF, placed([P, M_HALF], F32, "last_body2", 108)[:])
+        def y_max(m0, ox_sums, rd_sums):
+            tile = res[(m0, ox_sums)]
+            count, width = tile.shape[1], tile.shape[2]
+            first = len(rd_sums) - count
+            n0 = ox_sums[0][1] * P
+            nc.vector.tensor_tensor(tile[:], y_ps[(m0, rd_sums)][:, first : first + count, :], tile[:], MAX)
+            nc.sync.dma_start(out[n0 : n0 + count * P, m0 : m0 + width].rearrange("(u p) m -> p u m", u=count), tile[:])
+
+        def run_of(style, n0, count):
+            return tuple((style, n) for n in range(n0, n0 + count))
+
+        pairs = [(run_of(OX, n0, 2), run_of(RD, n0, 2)) for n0 in range(0, N_TILES, 2)]
+        mixed = run_of(OX, 4, 2) + run_of(RD, 4, 2)
+        fours = [(run_of(OX, 0, 4), run_of(RD, 0, 4)), (mixed, mixed)]
+        quarter_banks = [fours[0][0], fours[0][1], mixed]
+        m_b, m_c = HALF, HALF + QUARTER
+        half_banks = [pair[style] for style in (OX, RD) for pair in pairs]
+        for sums in half_banks:
+            open_bank(0, HALF, sums)
+        for m0 in (m_b, m_c):
+            for sums in quarter_banks:
+                open_bank(m0, QUARTER, sums)
+        for sums in half_banks:
+            y_pass(0, 0, sums)
+        for sums in quarter_banks[0:2]:
+            y_pass(0, m_b, sums)
+
+        for g in late_tiles:
+            gained_square(g, 0)
+        for g in late_tiles[1:]:
+            pick_rim(g, HALF)
+        round_z(1, 0, damp[(1, 0)][:], 84)
+        pick_body(4, m_b, QUARTER)
+        square(damp[(1, HALF)][:])
+        pick_body(5, m_b, QUARTER)
+        pick_body(6, m_b, QUARTER)
+        inverse_root(damp[(1, HALF)][:])
+        pick_body(7, m_b, QUARTER)
+        pick_base(4, m_b)
         quantize_z(1, 0)
-        pick_base(7, M_HALF, M_HALF)
-        last_order = ((0, OX), (1, OX), (0, RD), (2, OX), (1, RD), (2, RD))
-        for pair, style in last_order:
-            y_pass(1, 0, pair, style)
-        round_z(1, M_HALF, M_HALF, z_rounded[(1, M_HALF)][:])
-        y_out(0, 0)
-        quantize_z(1, M_HALF)
-        for pair in range(1, PAIRS):
-            y_out(0, pair)
-        for style in (OX, RD):
-            y_pass(0, M_HALF, 1, style)
-        for pair, style in last_order:
-            if pair == PAIRS - 1:
-                y_pass(0, M_HALF, pair, style)
-            y_pass(1, M_HALF, pair, style)
-        for pair in range(PAIRS):
-            y_out(M_HALF, pair, 2 if pair == PAIRS - 1 else 1)
+        pick_base(5, m_b)
+        pick_base(6, m_b)
+        for pair in pairs:
+            y_pass(1, 0, pair[OX])
+            y_pass(1, 0, pair[RD])
+        for g in late_tiles:
+            gained_square(g, HALF)
+        pick_base(7, m_b)
+        y_copy(0, pairs[0][OX], 16)
+        pick_body(4, m_c, QUARTER)
+        pick_body(5, m_c, QUARTER)
+        y_copy(0, pairs[1][OX], 18)
+        pick_body(6, m_c, QUARTER)
+        pick_body(7, m_c, QUARTER)
+        y_copy(0, pairs[2][OX], 20)
+        y_pass(0, m_b, mixed)
+        y_max(0, *pairs[0])
+        round_z(1, m_b, damp[(1, HALF)][:, :, 0:QUARTER], 86)
+        pick_base(4, m_c)
+        pick_base(5, m_c)
+        quantize_z(1, m_b)
+        pick_base(6, m_c)
+        pick_base(7, m_c)
+        for sums in quarter_banks:
+            y_pass(1, m_b, sums)
+        for sums in quarter_banks:
+            y_pass(0, m_c, sums)
+        y_max(0, *pairs[1])
+        round_z(1, m_c, damp[(1, HALF)][:, :, QUARTER:HALF], 87)
+        y_max(0, *pairs[2])
+        quantize_z(1, m_c)
+        for sums in quarter_banks:
+            y_pass(1, m_c, sums)
+        for i, m0 in enumerate((m_b, m_c)):
+            y_copy(m0, fours[0][0], 22 + 3 * i)
+            y_copy(m0, mixed, 24 + 3 * i)
+            y_max(m0, *fours[0])
+            y_max(m0, *fours[1])

@@ -96,10 +96,10 @@ def tile_list_sherd_vessel_joining_kernel(
         v_w = [kept([P, S], U32, "v_w%d" % a) for a in range(K_PASSES)]
         v_sc = kept([P, S], U8, "v_sc")
 
-        def quantize(name, rounded):
+        def quantize(name, rounded, kib=None):
             width = rounded.shape[1] // PACK
             scales = kept([P, width], U8, name + "_scales")
-            codes = kept([P, width], U32, name + "_codes")
+            codes = kept([P, width], U32, name + "_codes") if kib is None else placed([P, width], U32, name + "_codes", kib)
             nc.vector.quantize_mx(out=codes[:].bitcast(FP8X4), scales=scales[:], in_=rounded)
             return codes, scales
 
@@ -163,7 +163,7 @@ def tile_list_sherd_vessel_joining_kernel(
                 wox_scales[:, 4 * q : 4 * q + 4, :].rearrange("b r n -> r b n").bitcast(I32),
             )
 
-        late = [kept([P, PACK * PASS], BF16, "late%d" % a) for a in range(K_PASSES)]
+        late = [placed([P, PACK * PASS], BF16, "late%d" % a, 114 - 4 * a) for a in range(K_PASSES)]
 
         def round_late(a):
             for u in range(2):
@@ -172,64 +172,47 @@ def tile_list_sherd_vessel_joining_kernel(
         def quantize_late(a):
             quantize_w1("late%d" % a, late[a][:], a, range(PACK, 2 * PACK))
 
-        wrd_rounded, wrd_q = {}, {}
+        wrd_rounded = placed([P, R_PASSES * PACK * N], BF16, "wrd_rounded", 60)
+        wrd_q = []
 
         def round_wrd(b):
-            wrd_rounded[b] = placed([P, PACK * N], BF16, "wrd_rounded%d" % b, (88, 56)[b])
             nc.vector.tensor_copy(
-                wrd_rounded[b][:].rearrange("p (c i j) -> p c j i", i=LINE, j=PACK),
+                wrd_rounded[:, b * PACK * N : (b + 1) * PACK * N].rearrange("p (c i j) -> p c j i", i=LINE, j=PACK),
                 wrd_raw[b][:].rearrange("p j (c i) -> p c j i", i=LINE),
             )
 
-        def quantize_wrd(b):
-            half = PACK * N // 2
-            wrd_q[b] = [
-                block
-                for c in (0, half)
-                for block in blocks(quantize("wrd_%d_%d" % (b, c), wrd_rounded[b][:, c : c + half]))
-            ]
+        def quantize_wrd(c0, width, kib=None):
+            wrd_q.extend(blocks(quantize("wrd_%d" % c0, wrd_rounded[:, c0 : c0 + width], kib)))
 
-        damp = {
-            (0, 0): placed([P, PACK, M], F32, "damp0", 56),
-            (1, 0): placed([P, PACK, HALF], F32, "damp1a", 72),
-            (1, HALF): placed([P, PACK, HALF], F32, "damp1b", 76),
-        }
-        prod = {
-            (0, 0): placed([P, PACK, M], F32, "prod0", 48),
-            (1, 0): placed([P, PACK, HALF], F32, "prod1a", 64),
-            (1, HALF): placed([P, PACK, QUARTER], F32, "prod1b", 68),
-            (1, HALF + QUARTER): placed([P, PACK, QUARTER], F32, "prod1c", 70),
-        }
         body, z_rounded, z_q = {}, {}, {}
 
-        def pick_body(g, m0, width, pick=scalar_pick):
-            body[(g, m0)] = kept([P, width], F32, "body%d_%d" % (g, m0))
-            pick(body[(g, m0)][:], picked(g, BODY, m0, width))
+        def pick_body(g, m0, width, kib=None):
+            name = "body%d_%d" % (g, m0)
+            body[(g, m0)] = kept([P, width], F32, name) if kib is None else placed([P, width], F32, name, kib)
+            scalar_pick(body[(g, m0)][:], picked(g, BODY, m0, width))
 
-        def pick_rim(g, m0, pick=scalar_pick):
-            dst = damp[(g // PACK, m0)][:, g % PACK, :]
-            pick(dst, picked(g, RIM, m0, dst.shape[1]))
+        def pick_rim(g, m0, rims, pick=scalar_pick):
+            pick(rims[:, g % PACK, :], picked(g, RIM, m0, rims.shape[2]))
 
-        def pick_base(g, m0):
-            dst = prod[(g // PACK, m0)][:, g % PACK, :]
+        def pick_base(g, m0, products):
+            dst = products[:, g % PACK, :]
             nc.vector.tensor_tensor(dst, picked(g, BASE, m0, dst.shape[1]), body[(g, m0)][:], MULT)
 
-        def square(x):
-            nc.scalar.activation(x, x, ACT.Square)
+        def square(dst, src):
+            nc.scalar.activation(dst, src, ACT.Square)
 
-        def inverse_root(x):
-            nc.scalar.activation(x, x, ACT.Abs_reciprocal_sqrt, bias=1.0)
+        def inverse_root(dst, src):
+            nc.scalar.activation(dst, src, ACT.Abs_reciprocal_sqrt, bias=1.0)
 
-        def gained_square(g, m0):
-            x = damp[(g // PACK, m0)][:, g % PACK, :]
-            nc.vector.scalar_tensor_tensor(x, x, gain_t[:, g : g + 1], x, MULT, MULT)
+        def gained_square(g, gained, roots):
+            root = roots[:, g % PACK, :]
+            nc.vector.scalar_tensor_tensor(gained[:, g % PACK, :], root, gain_t[:, g : g + 1], root, MULT, MULT)
 
-        def round_z(b, m0, damping, kib):
-            width = prod[(b, m0)].shape[2]
-            z_rounded[(b, m0)] = placed([P, PACK * width], BF16, "z_rounded%d_%d" % (b, m0), kib)
+        def round_z(b, m0, products, damping, kib):
+            z_rounded[(b, m0)] = placed([P, PACK * damping.shape[2]], BF16, "z_rounded%d_%d" % (b, m0), kib)
             nc.vector.tensor_tensor(
                 z_rounded[(b, m0)][:].rearrange("p (c i t) -> p c t i", i=LINE, t=PACK),
-                prod[(b, m0)][:].rearrange("p t (c i) -> p c t i", i=LINE),
+                products.rearrange("p t (c i) -> p c t i", i=LINE),
                 damping.rearrange("p t (c i) -> p c t i", i=LINE),
                 MULT,
             )
@@ -237,68 +220,76 @@ def tile_list_sherd_vessel_joining_kernel(
         def quantize_z(b, m0):
             z_q[(b, m0)] = quantize("z_%d_%d" % (b, m0), z_rounded[(b, m0)][:])
 
+        late_tiles = range(PACK, 2 * PACK)
+        roots = placed([P, PACK, M], F32, "roots0", 48)
+        prod0 = placed([P, PACK, M], F32, "prod0", 90)
+        rims23 = placed([P, 2, M], F32, "rims23", 86)
+        for a in range(K_PASSES):
+            round_late(a)
         h_out(0, 0)
         h_out(0, 1)
         h_out(1, 0)
         pick_body(0, 0, M)
-        round_late(0)
-        pick_rim(0, 0, nc.vector.tensor_copy)
+        pick_rim(0, 0, roots, nc.vector.tensor_copy)
         quantize_late(0)
         h_out(1, 1)
         h_out(2, 0)
-        pick_base(0, 0)
-        round_late(1)
         pick_body(1, 0, M)
-        pick_rim(1, 0)
-        pick_base(1, 0)
-        quantize_late(1)
         h_out(2, 1)
-        round_late(2)
+        pick_rim(1, 0, roots)
+        quantize_late(1)
+        quantize_late(2)
+        pick_base(0, 0, prod0)
+        pick_base(1, 0, prod0)
+        nc.vector.tensor_copy(rims23[:, 0, :], picked(2, RIM, 0, M))
         h_out(3, 0)
         pick_body(2, 0, M)
-        pick_rim(2, 0, nc.vector.tensor_copy)
-        quantize_late(2)
-        for g in range(PACK, 2 * PACK):
+        for g in late_tiles:
             for bank in range(S // BANK):
                 for a in range(K_PASSES):
                     h_pass(g, bank, a)
+        square(roots[:, 0:2, :], roots[:, 0:2, :])
         h_out(3, 1)
-        square(damp[(0, 0)][:, 0:2, :])
-        pick_base(2, 0)
-        pick_rim(3, 0)
-        inverse_root(damp[(0, 0)][:, 0:2, :])
+        inverse_root(roots[:, 0:2, :], roots[:, 0:2, :])
+        pick_base(2, 0, prod0)
+        scalar_pick(rims23[:, 1, :], picked(3, RIM, 0, M))
         pick_body(3, 0, M)
-        square(damp[(0, 0)][:, 2:PACK, :])
-        round_wrd(0)
+        square(roots[:, 2:PACK, :], rims23[:])
         h_out(4, 0)
-        pick_base(3, 0)
-        inverse_root(damp[(0, 0)][:, 2:PACK, :])
-        gained_square(0, 0)
-        gained_square(1, 0)
-        quantize_wrd(0)
-        gained_square(2, 0)
-        gained_square(3, 0)
-        round_z(0, 0, damp[(0, 0)][:], 80)
+        inverse_root(roots[:, 2:PACK, :], roots[:, 2:PACK, :])
+        gained0 = placed([P, PACK, M], F32, "gained0", 106)
+        gained_square(0, gained0, roots)
+        gained_square(1, gained0, roots)
+        pick_base(3, 0, prod0)
+        gained_square(2, gained0, roots)
+        gained_square(3, gained0, roots)
+        round_wrd(0)
+        round_z(0, 0, prod0[:], gained0[:], 56)
+        round_wrd(1)
+        quantize_z(0, 0)
+        quantize_wrd(0, 4096)
+        quantize_wrd(4096, 2048)
 
-        late_tiles = range(PACK, 2 * PACK)
+        m_b, m_c = HALF, HALF + QUARTER
+        rims_a = placed([P, PACK, HALF], F32, "rims_a", 98)
+        squares_a = placed([P, PACK, HALF], F32, "squares_a", 102)
+        roots_a = placed([P, PACK, HALF], F32, "roots_a", 72)
+        prod_a = placed([P, PACK, HALF], F32, "prod_a", 30)
+        gained_a = placed([P, PACK, HALF], F32, "gained_a", 36)
         h_out(4, 1)
         for g in late_tiles[:-1]:
             h_out(g + 1, 0)
-            pick_rim(g, 0)
             h_out(g + 1, 1)
-            pick_body(g, 0, HALF)
-        pick_rim(7, 0)
+            pick_rim(g, 0, rims_a)
+        pick_rim(7, 0, rims_a)
+        pick_body(4, 0, HALF)
+        pick_body(5, 0, HALF)
+        pick_body(6, 0, HALF)
+        square(squares_a[:], rims_a[:])
         pick_body(7, 0, HALF)
-        pick_base(4, 0)
-        quantize_z(0, 0)
-        pick_base(5, 0)
-        round_wrd(1)
-        pick_base(6, 0)
-        pick_base(7, 0)
-        quantize_wrd(1)
-        square(damp[(1, 0)][:])
-        pick_rim(4, HALF)
-        inverse_root(damp[(1, 0)][:])
+        inverse_root(roots_a[:], squares_a[:])
+        for g in late_tiles[:-1]:
+            pick_base(g, 0, prod_a)
 
         y_ps = {}
 
@@ -314,7 +305,7 @@ def tile_list_sherd_vessel_joining_kernel(
                 if style == OX:
                     codes, scales = wox_w[:, b, 2 * n * P : 2 * (n + 1) * P].bitcast(FP4X4), wox_sc[:, b, n * P : (n + 1) * P]
                 else:
-                    codes, scales = wrd_q[b][n][0].bitcast(FP8X4), wrd_q[b][n][1]
+                    codes, scales = wrd_q[b * N_TILES + n][0].bitcast(FP8X4), wrd_q[b * N_TILES + n][1]
                 nc.tensor.matmul_mx(
                     out=bank[:, u, :],
                     lhsT=codes,
@@ -348,7 +339,6 @@ def tile_list_sherd_vessel_joining_kernel(
         mixed = run_of(OX, 4, 2) + run_of(RD, 4, 2)
         fours = [(run_of(OX, 0, 4), run_of(RD, 0, 4)), (mixed, mixed)]
         quarter_banks = [fours[0][0], fours[0][1], mixed]
-        m_b, m_c = HALF, HALF + QUARTER
         half_banks = [pair[style] for style in (OX, RD) for pair in pairs]
         for sums in half_banks:
             open_bank(0, HALF, sums)
@@ -360,54 +350,63 @@ def tile_list_sherd_vessel_joining_kernel(
         for sums in quarter_banks[0:2]:
             y_pass(0, m_b, sums)
 
+        for g in late_tiles[:-1]:
+            gained_square(g, gained_a, roots_a)
+        pick_base(7, 0, prod_a)
+        gained_square(7, gained_a, roots_a)
+
+        rims_b = placed([P, PACK, HALF], F32, "rims_b", 98)
+        squares_b = placed([P, PACK, HALF], F32, "squares_b", 88)
+        roots_b = placed([P, PACK, HALF], F32, "roots_b", 76)
+        prod_b = placed([P, PACK, QUARTER], F32, "prod_b", 37)
+        prod_c = placed([P, PACK, QUARTER], F32, "prod_c", 38.5)
+        gained_b = placed([P, PACK, HALF], F32, "gained_b", 30)
         for g in late_tiles:
-            gained_square(g, 0)
-        for g in late_tiles[1:]:
-            pick_rim(g, HALF)
-        round_z(1, 0, damp[(1, 0)][:], 84)
-        pick_body(4, m_b, QUARTER)
-        square(damp[(1, HALF)][:])
-        pick_body(5, m_b, QUARTER)
-        pick_body(6, m_b, QUARTER)
-        inverse_root(damp[(1, HALF)][:])
-        pick_body(7, m_b, QUARTER)
-        pick_base(4, m_b)
+            pick_rim(g, HALF, rims_b)
+        pick_body(4, m_b, QUARTER, 102)
+        square(squares_b[:], rims_b[:])
+        pick_body(5, m_b, QUARTER, 98)
+        inverse_root(roots_b[:], squares_b[:])
+        pick_body(6, m_b, QUARTER, 88)
+        pick_body(7, m_b, QUARTER, 88.5)
+        round_z(1, 0, prod_a[:], gained_a[:], 80)
         quantize_z(1, 0)
-        pick_base(5, m_b)
-        pick_base(6, m_b)
+        pick_base(4, m_b, prod_b)
+        pick_base(5, m_b, prod_b)
         for pair in pairs:
             y_pass(1, 0, pair[OX])
             y_pass(1, 0, pair[RD])
-        for g in late_tiles:
-            gained_square(g, HALF)
-        pick_base(7, m_b)
-        y_copy(0, pairs[0][OX], 16)
-        pick_body(4, m_c, QUARTER)
-        pick_body(5, m_c, QUARTER)
-        y_copy(0, pairs[1][OX], 18)
-        pick_body(6, m_c, QUARTER)
-        pick_body(7, m_c, QUARTER)
-        y_copy(0, pairs[2][OX], 20)
-        y_pass(0, m_b, mixed)
-        y_max(0, *pairs[0])
-        round_z(1, m_b, damp[(1, HALF)][:, :, 0:QUARTER], 86)
-        pick_base(4, m_c)
-        pick_base(5, m_c)
+        last_body = placed([P, PACK, QUARTER], F32, "last_body", 89)
+        last_base = placed([P, PACK, QUARTER], F32, "last_base", 91)
+        for which, tile in ((BODY, last_body), (BASE, last_base)):
+            for g in late_tiles:
+                scalar_pick(tile[:, g % PACK, :], picked(g, which, m_c, QUARTER))
+        for g in late_tiles[:-1]:
+            gained_square(g, gained_b, roots_b)
+        pick_base(6, m_b, prod_b)
+        pick_base(7, m_b, prod_b)
+        gained_square(7, gained_b, roots_b)
+        round_z(1, m_b, prod_b[:], gained_b[:, :, 0:QUARTER], 82)
+        nc.vector.tensor_tensor(prod_c[:], last_base[:], last_body[:], MULT)
         quantize_z(1, m_b)
-        pick_base(6, m_c)
-        pick_base(7, m_c)
+        round_z(1, m_c, prod_c[:], gained_b[:, :, QUARTER:HALF], 85)
+        quantize_z(1, m_c)
+        for i, pair in enumerate(pairs):
+            y_copy(0, pair[OX], (35.5, 80.5, 82.5)[i])
+        y_pass(0, m_b, mixed)
         for sums in quarter_banks:
             y_pass(1, m_b, sums)
         for sums in quarter_banks:
             y_pass(0, m_c, sums)
-        y_max(0, *pairs[1])
-        round_z(1, m_c, damp[(1, HALF)][:, :, QUARTER:HALF], 87)
-        y_max(0, *pairs[2])
-        quantize_z(1, m_c)
+        for pair in pairs:
+            y_max(0, *pair)
+        y_copy(m_b, fours[0][0], 22)
+        y_copy(m_b, mixed, 24)
+        y_max(m_b, *fours[0])
+        y_max(m_b, *fours[1])
         for sums in quarter_banks:
             y_pass(1, m_c, sums)
-        for i, m0 in enumerate((m_b, m_c)):
-            y_copy(m0, fours[0][0], 22 + 3 * i)
-            y_copy(m0, mixed, 24 + 3 * i)
-            y_max(m0, *fours[0])
-            y_max(m0, *fours[1])
+        y_copy(m_c, fours[0][0], 25)
+        y_copy(m_c, mixed, 27)
+        y_max(m_c, *fours[0])
+        y_max(m_c, *fours[1])

@@ -163,14 +163,13 @@ def tile_list_sherd_vessel_joining_kernel(
                 wox_scales[:, 4 * q : 4 * q + 4, :].rearrange("b r n -> r b n").bitcast(I32),
             )
 
-        late = [placed([P, PACK * PASS], BF16, "late%d" % a, 114 - 4 * a) for a in range(K_PASSES)]
+        late_first = kept([P, PACK * PASS], BF16, "late_first")
+        late_rest = placed([P, K_PASSES - 1, PACK * PASS], BF16, "late_rest", 106)
 
         def round_late(a):
+            dst = late_first[:] if a == 0 else late_rest[:, a - 1, :]
             for u in range(2):
-                round_w1(1, a, u, late[a][:, 2 * u * PASS : 2 * (u + 1) * PASS], nc.vector.tensor_copy)
-
-        def quantize_late(a):
-            quantize_w1("late%d" % a, late[a][:], a, range(PACK, 2 * PACK))
+                round_w1(1, a, u, dst[:, 2 * u * PASS : 2 * (u + 1) * PASS], nc.vector.tensor_copy)
 
         wrd_rounded = placed([P, R_PASSES * PACK * N], BF16, "wrd_rounded", 60)
         wrd_q = []
@@ -222,44 +221,43 @@ def tile_list_sherd_vessel_joining_kernel(
 
         late_tiles = range(PACK, 2 * PACK)
         roots = placed([P, PACK, M], F32, "roots0", 48)
-        prod0 = placed([P, PACK, M], F32, "prod0", 90)
-        rims23 = placed([P, 2, M], F32, "rims23", 86)
+        prod0 = placed([P, PACK, M], F32, "prod0", 88)
         for a in range(K_PASSES):
             round_late(a)
         h_out(0, 0)
         h_out(0, 1)
         h_out(1, 0)
-        pick_body(0, 0, M)
-        pick_rim(0, 0, roots, nc.vector.tensor_copy)
-        quantize_late(0)
         h_out(1, 1)
-        h_out(2, 0)
-        pick_body(1, 0, M)
-        h_out(2, 1)
-        pick_rim(1, 0, roots)
-        quantize_late(1)
-        quantize_late(2)
-        pick_base(0, 0, prod0)
-        pick_base(1, 0, prod0)
-        nc.vector.tensor_copy(rims23[:, 0, :], picked(2, RIM, 0, M))
-        h_out(3, 0)
-        pick_body(2, 0, M)
+        pick_rim(0, 0, roots, nc.vector.tensor_copy)
+        quantize_w1("late_first", late_first[:], 0, late_tiles)
+        pick_rim(1, 0, roots, nc.vector.tensor_copy)
+        for i, block in enumerate(blocks(quantize("late_rest", late_rest[:].rearrange("p a c -> p (a c)")))):
+            w1_q[(PACK + i % PACK, 1 + i // PACK)] = block
         for g in late_tiles:
             for bank in range(S // BANK):
                 for a in range(K_PASSES):
                     h_pass(g, bank, a)
+        pick_body(0, 0, M)
+        h_out(2, 0)
+        h_out(2, 1)
+        pick_rim(2, 0, roots, nc.vector.tensor_copy)
+        pick_body(1, 0, M)
         square(roots[:, 0:2, :], roots[:, 0:2, :])
-        h_out(3, 1)
+        h_out(3, 0)
         inverse_root(roots[:, 0:2, :], roots[:, 0:2, :])
-        pick_base(2, 0, prod0)
-        scalar_pick(rims23[:, 1, :], picked(3, RIM, 0, M))
-        pick_body(3, 0, M)
-        square(roots[:, 2:PACK, :], rims23[:])
+        h_out(3, 1)
+        pick_body(2, 0, M)
+        pick_rim(3, 0, roots)
         h_out(4, 0)
+        square(roots[:, 2:PACK, :], roots[:, 2:PACK, :])
+        pick_body(3, 0, M)
         inverse_root(roots[:, 2:PACK, :], roots[:, 2:PACK, :])
+        pick_base(0, 0, prod0)
+        pick_base(1, 0, prod0)
         gained0 = placed([P, PACK, M], F32, "gained0", 106)
         gained_square(0, gained0, roots)
         gained_square(1, gained0, roots)
+        pick_base(2, 0, prod0)
         pick_base(3, 0, prod0)
         gained_square(2, gained0, roots)
         gained_square(3, gained0, roots)
@@ -268,10 +266,9 @@ def tile_list_sherd_vessel_joining_kernel(
         round_wrd(1)
         quantize_z(0, 0)
         quantize_wrd(0, 4096)
-        quantize_wrd(4096, 2048)
 
         m_b, m_c = HALF, HALF + QUARTER
-        rims_a = placed([P, PACK, HALF], F32, "rims_a", 98)
+        rims_a = placed([P, PACK, HALF], F32, "rims_a", 44)
         squares_a = placed([P, PACK, HALF], F32, "squares_a", 102)
         roots_a = placed([P, PACK, HALF], F32, "roots_a", 72)
         prod_a = placed([P, PACK, HALF], F32, "prod_a", 30)
@@ -286,10 +283,13 @@ def tile_list_sherd_vessel_joining_kernel(
         pick_body(5, 0, HALF)
         pick_body(6, 0, HALF)
         square(squares_a[:], rims_a[:])
-        pick_body(7, 0, HALF)
+        pick_body(7, 0, HALF, 98)
         inverse_root(roots_a[:], squares_a[:])
+        rims_b = placed([P, PACK, HALF], F32, "rims_b", 42)
         for g in late_tiles[:-1]:
             pick_base(g, 0, prod_a)
+        for g in late_tiles[0:1]:
+            pick_rim(g, HALF, rims_b, nc.vector.tensor_copy)
 
         y_ps = {}
 
@@ -354,18 +354,18 @@ def tile_list_sherd_vessel_joining_kernel(
             gained_square(g, gained_a, roots_a)
         pick_base(7, 0, prod_a)
         gained_square(7, gained_a, roots_a)
+        quantize_wrd(4096, 2048, 98.5)
 
-        rims_b = placed([P, PACK, HALF], F32, "rims_b", 98)
         squares_b = placed([P, PACK, HALF], F32, "squares_b", 88)
         roots_b = placed([P, PACK, HALF], F32, "roots_b", 76)
-        prod_b = placed([P, PACK, QUARTER], F32, "prod_b", 37)
-        prod_c = placed([P, PACK, QUARTER], F32, "prod_c", 38.5)
+        prod_b = placed([P, PACK, QUARTER], F32, "prod_b", 36)
+        prod_c = placed([P, PACK, QUARTER], F32, "prod_c", 38)
         gained_b = placed([P, PACK, HALF], F32, "gained_b", 30)
-        for g in late_tiles:
+        for g in late_tiles[1:]:
             pick_rim(g, HALF, rims_b)
         pick_body(4, m_b, QUARTER, 102)
         square(squares_b[:], rims_b[:])
-        pick_body(5, m_b, QUARTER, 98)
+        pick_body(5, m_b, QUARTER, 42)
         inverse_root(roots_b[:], squares_b[:])
         pick_body(6, m_b, QUARTER, 88)
         pick_body(7, m_b, QUARTER, 88.5)
@@ -376,30 +376,31 @@ def tile_list_sherd_vessel_joining_kernel(
         for pair in pairs:
             y_pass(1, 0, pair[OX])
             y_pass(1, 0, pair[RD])
-        last_body = placed([P, PACK, QUARTER], F32, "last_body", 89)
-        last_base = placed([P, PACK, QUARTER], F32, "last_base", 91)
-        for which, tile in ((BODY, last_body), (BASE, last_base)):
-            for g in late_tiles:
-                scalar_pick(tile[:, g % PACK, :], picked(g, which, m_c, QUARTER))
+        for g in late_tiles:
+            pick_body(g, m_c, QUARTER, 89 + 0.5 * (g % PACK))
+        for i, pair in enumerate(pairs):
+            y_copy(0, pair[OX], 16 + 2 * i)
         for g in late_tiles[:-1]:
             gained_square(g, gained_b, roots_b)
         pick_base(6, m_b, prod_b)
         pick_base(7, m_b, prod_b)
         gained_square(7, gained_b, roots_b)
+        pick_base(4, m_c, prod_c)
         round_z(1, m_b, prod_b[:], gained_b[:, :, 0:QUARTER], 82)
-        nc.vector.tensor_tensor(prod_c[:], last_base[:], last_body[:], MULT)
+        pick_base(5, m_c, prod_c)
         quantize_z(1, m_b)
+        pick_base(6, m_c, prod_c)
+        pick_base(7, m_c, prod_c)
+        y_max(0, *pairs[0])
         round_z(1, m_c, prod_c[:], gained_b[:, :, QUARTER:HALF], 85)
+        y_max(0, *pairs[1])
         quantize_z(1, m_c)
-        for i, pair in enumerate(pairs):
-            y_copy(0, pair[OX], (35.5, 80.5, 82.5)[i])
+        y_max(0, *pairs[2])
         y_pass(0, m_b, mixed)
         for sums in quarter_banks:
             y_pass(1, m_b, sums)
         for sums in quarter_banks:
             y_pass(0, m_c, sums)
-        for pair in pairs:
-            y_max(0, *pair)
         y_copy(m_b, fours[0][0], 22)
         y_copy(m_b, mixed, 24)
         y_max(m_b, *fours[0])

@@ -60,31 +60,39 @@ def tile_list_sherd_vessel_joining_kernel(
             nc.sync.dma_start(tile[:], entries)
             return tile
 
-        def load_table(a, kib):
-            words = placed([P, T], U32, "tab_w%d" % a, kib)
-            nc.sync.dma_start(words[:].bitcast(I32), tab_words[a].rearrange("p t i -> p (t i)").bitcast(I32))
-            return words
+        def load_words(a, c0, c1):
+            src = tab_words[a].rearrange("p t i -> p (t i)").bitcast(I32)
+            nc.sync.dma_start(tab_w[a][:, c0:c1].bitcast(I32), src[:, c0:c1])
 
-        tab_sc = kept([P, T], U8, "tab_sc")
-        wox_sc = kept([P, R_PASSES, N], U8, "wox_sc")
-        nc.vector.memset(tab_sc[:].bitcast(I32), 0)
-        nc.vector.memset(wox_sc[:].rearrange("p b n -> p (b n)").bitcast(I32), 0)
+        tab_sc = [placed([P, T], U8, "tab_sc%d" % a, (96, 100, 46)[a]) for a in range(K_PASSES)]
+        v_sc = kept([P, K_PASSES, S], U8, "v_sc")
+        for tile in tab_sc:
+            nc.vector.memset(tile[:].bitcast(I32), 0)
+        nc.vector.memset(v_sc[:].rearrange("p a j -> p (a j)").bitcast(I32), 0)
 
-        raw, tab_w = {}, {}
-        tab_w[0] = load_table(0, 0)
+        raw = {}
+        tab_w = [placed([P, T], U32, "tab_w%d" % a, (16, 0, 32)[a]) for a in range(K_PASSES)]
+        load_words(0, 0, T // 2)
         offs_t = load_list(offs, "offs_t")
-        for q in range(QUADRANTS):
+        for a in range(K_PASSES):
+            nc.sync.dma_start(tab_sc[a][0:P:8, :].bitcast(I32), tab_scales[a].bitcast(I32))
+        load_words(0, T // 2, T)
+        raw[(0, 0)] = load_rows(w1, "w1_00", 0, 0, PASS, 88)
+        pos_t = [load_list(pos, "pos_t%d" % which) for which, pos in enumerate((pos1, pos2))]
+        load_words(1, 0, T)
+        pos_t.append(load_list(pos3, "pos_t2"))
+        raw[(0, 1)] = load_rows(w1, "w1_01", 1, 0, PASS, 114)
+
+        picked_sc = placed([P, K_PASSES, S], U8, "picked_sc", 78)
+        for a in range(K_PASSES):
+            nc.vector.tensor_copy(picked_sc[:, a, :], tab_sc[a][:].indirect(offs_t[:]))
+        for r in range(4):
             nc.sync.dma_start(
-                tab_sc[32 * q : 32 * q + 4 * K_PASSES, :].bitcast(I32),
-                tab_scales[:, 4 * q : 4 * q + 4, :].bitcast(I32),
+                v_sc[r:P:32].rearrange("p a j -> p (a j)").bitcast(I32),
+                picked_sc[8 * r : P : 32].rearrange("p a j -> p (a j)").bitcast(I32),
             )
-        for a in range(K_PASSES):
-            if a > 0:
-                tab_w[a] = load_table(a, (0, 32, 16)[a])
-            raw[(0, a)] = load_rows(w1, "w1_0%d" % a, a, 0, PASS, 48 + 8 * a)
-        pos_t = [load_list(pos, "pos_t%d" % which) for which, pos in enumerate((pos1, pos2, pos3))]
-        for a in range(K_PASSES):
-            raw[(1, a)] = load_rows(w1, "w1_1%d" % a, a, PASS, PASS, 72 + 8 * a)
+        load_words(2, 0, T)
+        raw[(0, 2)] = load_rows(w1, "w1_02", 2, 0, PASS, 48)
 
         gain_t = keep.tile([P, R_PASSES * PACK], F32, name="gain_t")
         nc.gpsimd.dma_start(
@@ -93,8 +101,7 @@ def tile_list_sherd_vessel_joining_kernel(
         warm = keep.tile([P, 1], F32, name="warm")
         nc.scalar.activation(warm[:], gain_t[:, 0:1], ACT.Abs_reciprocal_sqrt, bias=1.0, scale=0.0)
 
-        v_w = [kept([P, S], U32, "v_w%d" % a) for a in range(K_PASSES)]
-        v_sc = kept([P, S], U8, "v_sc")
+        v_w = [placed([P, S], U32, "v_w0", 96)] + [kept([P, S], U32, "v_w%d" % a) for a in range(1, K_PASSES)]
 
         def quantize(name, rounded, kib=None):
             width = rounded.shape[1] // PACK
@@ -127,7 +134,7 @@ def tile_list_sherd_vessel_joining_kernel(
                 lhsT=codes.bitcast(FP8X4),
                 lhsT_scale=scales,
                 rhs=v_w[a][:, cols].bitcast(FP8X4),
-                rhs_scale=v_sc[4 * a : P, cols],
+                rhs_scale=v_sc[:, a, cols],
                 start=(a == 0),
                 stop=(a == K_PASSES - 1),
             )
@@ -145,17 +152,19 @@ def tile_list_sherd_vessel_joining_kernel(
 
         for a in range(K_PASSES):
             nc.vector.tensor_copy(v_w[a][:], tab_w[a][:].indirect(offs_t[:]))
-            if a == 0:
-                nc.vector.tensor_copy(v_sc[:], tab_sc[:].indirect(offs_t[:]))
             for u in range(2):
                 rounded = ring.tile([P, 2 * PACK * P], BF16, name="narrow", tag="narrow", align_bytes=64)
-                round_w1(0, a, u, rounded[:], (nc.vector.tensor_copy, nc.scalar.copy)[u])
+                round_w1(0, a, u, rounded[:], nc.vector.tensor_copy if (a, u) == (K_PASSES - 1, 0) else nc.scalar.copy)
                 quantize_w1("w1_0%d%d" % (a, u), rounded[:], a, [2 * u, 2 * u + 1])
             for g in range(PACK):
                 for bank in range(S // BANK):
                     h_pass(g, bank, a)
+        for a in range(K_PASSES):
+            raw[(1, a)] = load_rows(w1, "w1_1%d" % a, a, PASS, PASS, (16, 24, 88)[a])
         wrd_raw = [load_rows(wrd, "wrd_raw%d" % b, b, 0, N, 32 * b) for b in range(R_PASSES)]
-        wox_w = kept([P, R_PASSES, 2 * N], U8, "wox_w")
+        wox_w = placed([P, R_PASSES, 2 * N], U8, "wox_w", 12)
+        wox_sc = placed([P, R_PASSES, N], U8, "wox_sc", 121)
+        nc.vector.memset(wox_sc[:].rearrange("p b n -> p (b n)").bitcast(I32), 0)
         nc.sync.dma_start(wox_w[:].bitcast(I32), wox_words.rearrange("b p c -> p b c").bitcast(I32))
         for q in range(QUADRANTS):
             nc.sync.dma_start(
@@ -379,7 +388,7 @@ def tile_list_sherd_vessel_joining_kernel(
         for g in late_tiles:
             pick_body(g, m_c, QUARTER, 89 + 0.5 * (g % PACK))
         for i, pair in enumerate(pairs):
-            y_copy(0, pair[OX], 16 + 2 * i)
+            y_copy(0, pair[OX], 17 + 2 * i)
         for g in late_tiles[:-1]:
             gained_square(g, gained_b, roots_b)
         pick_base(6, m_b, prod_b)
@@ -401,13 +410,13 @@ def tile_list_sherd_vessel_joining_kernel(
             y_pass(1, m_b, sums)
         for sums in quarter_banks:
             y_pass(0, m_c, sums)
-        y_copy(m_b, fours[0][0], 22)
-        y_copy(m_b, mixed, 24)
+        y_copy(m_b, fours[0][0], 23)
+        y_copy(m_b, mixed, 25)
         y_max(m_b, *fours[0])
         y_max(m_b, *fours[1])
         for sums in quarter_banks:
             y_pass(1, m_c, sums)
-        y_copy(m_c, fours[0][0], 25)
-        y_copy(m_c, mixed, 27)
+        y_copy(m_c, fours[0][0], 26)
+        y_copy(m_c, mixed, 28)
         y_max(m_c, *fours[0])
         y_max(m_c, *fours[1])

@@ -94,12 +94,9 @@ def tile_list_sherd_vessel_joining_kernel(
         load_words(2, 0, T)
         raw[(0, 2)] = load_rows(w1, "w1_02", 2, 0, PASS, 48)
 
-        gain_t = keep.tile([P, R_PASSES * PACK], F32, name="gain_t")
-        nc.gpsimd.dma_start(
-            gain_t[:].rearrange("p (b t) -> p b t", t=PACK), gain.rearrange("(b p t) -> p b t", b=R_PASSES, t=PACK)
-        )
-        warm = keep.tile([P, 1], F32, name="warm")
-        nc.scalar.activation(warm[:], gain_t[:, 0:1], ACT.Abs_reciprocal_sqrt, bias=1.0, scale=0.0)
+        warm = keep.tile([P, 2], F32, name="warm")
+        nc.vector.memset(warm[:], 0.0)
+        nc.scalar.activation(warm[:, 1:2], warm[:, 0:1], ACT.Abs_reciprocal_sqrt, bias=1.0)
 
         v_w = [placed([P, S], U32, "v_w0", 96)] + [kept([P, S], U32, "v_w%d" % a) for a in range(1, K_PASSES)]
 
@@ -155,7 +152,11 @@ def tile_list_sherd_vessel_joining_kernel(
             for u in range(2):
                 rounded = ring.tile([P, 2 * PACK * P], BF16, name="narrow", tag="narrow", align_bytes=64)
                 round_w1(0, a, u, rounded[:], nc.vector.tensor_copy if (a, u) == (K_PASSES - 1, 0) else nc.scalar.copy)
-                quantize_w1("w1_0%d%d" % (a, u), rounded[:], a, [2 * u, 2 * u + 1])
+                if (a, u) == (K_PASSES - 1, 0):
+                    for s in range(2):
+                        quantize_w1("w1_last%d" % s, rounded[:, s * PASS : (s + 1) * PASS], a, [s])
+                else:
+                    quantize_w1("w1_0%d%d" % (a, u), rounded[:], a, [2 * u, 2 * u + 1])
             for g in range(PACK):
                 for bank in range(S // BANK):
                     h_pass(g, bank, a)
@@ -163,8 +164,12 @@ def tile_list_sherd_vessel_joining_kernel(
             raw[(1, a)] = load_rows(w1, "w1_1%d" % a, a, PASS, PASS, (16, 24, 88)[a])
         wrd_raw = [load_rows(wrd, "wrd_raw%d" % b, b, 0, N, 32 * b) for b in range(R_PASSES)]
         wox_w = placed([P, R_PASSES, 2 * N], U8, "wox_w", 12)
-        wox_sc = placed([P, R_PASSES, N], U8, "wox_sc", 121)
+        wox_sc = placed([P, R_PASSES, N], U8, "wox_sc", 120)
         nc.vector.memset(wox_sc[:].rearrange("p b n -> p (b n)").bitcast(I32), 0)
+        gain_t = placed([P, R_PASSES * PACK], F32, "gain_t", 121.5)
+        nc.sync.dma_start(
+            gain_t[:].rearrange("p (b t) -> p b t", t=PACK), gain.rearrange("(b p t) -> p b t", b=R_PASSES, t=PACK)
+        )
         nc.sync.dma_start(wox_w[:].bitcast(I32), wox_words.rearrange("b p c -> p b c").bitcast(I32))
         for q in range(QUADRANTS):
             nc.sync.dma_start(
@@ -367,49 +372,41 @@ def tile_list_sherd_vessel_joining_kernel(
 
         squares_b = placed([P, PACK, HALF], F32, "squares_b", 88)
         roots_b = placed([P, PACK, HALF], F32, "roots_b", 76)
-        prod_b = placed([P, PACK, QUARTER], F32, "prod_b", 36)
-        prod_c = placed([P, PACK, QUARTER], F32, "prod_c", 38)
+        prod_b = placed([P, PACK, HALF], F32, "prod_b", 36)
         gained_b = placed([P, PACK, HALF], F32, "gained_b", 30)
         for g in late_tiles[1:]:
             pick_rim(g, HALF, rims_b)
-        pick_body(4, m_b, QUARTER, 102)
+        pick_body(4, HALF, HALF, 102)
         square(squares_b[:], rims_b[:])
-        pick_body(5, m_b, QUARTER, 42)
+        pick_body(5, HALF, HALF, 103)
         inverse_root(roots_b[:], squares_b[:])
-        pick_body(6, m_b, QUARTER, 88)
-        pick_body(7, m_b, QUARTER, 88.5)
+        pick_body(6, HALF, HALF, 88)
+        pick_body(7, HALF, HALF, 89)
         round_z(1, 0, prod_a[:], gained_a[:], 80)
         quantize_z(1, 0)
-        pick_base(4, m_b, prod_b)
-        pick_base(5, m_b, prod_b)
+        pick_base(4, HALF, prod_b)
+        pick_base(5, HALF, prod_b)
         for pair in pairs:
             y_pass(1, 0, pair[OX])
             y_pass(1, 0, pair[RD])
-        for g in late_tiles:
-            pick_body(g, m_c, QUARTER, 89 + 0.5 * (g % PACK))
         for i, pair in enumerate(pairs):
             y_copy(0, pair[OX], 17 + 2 * i)
-        for g in late_tiles[:-1]:
+        for g in late_tiles:
             gained_square(g, gained_b, roots_b)
-        pick_base(6, m_b, prod_b)
-        pick_base(7, m_b, prod_b)
-        gained_square(7, gained_b, roots_b)
-        pick_base(4, m_c, prod_c)
-        round_z(1, m_b, prod_b[:], gained_b[:, :, 0:QUARTER], 82)
-        pick_base(5, m_c, prod_c)
-        quantize_z(1, m_b)
-        pick_base(6, m_c, prod_c)
-        pick_base(7, m_c, prod_c)
+        pick_base(6, HALF, prod_b)
+        pick_base(7, HALF, prod_b)
         y_max(0, *pairs[0])
-        round_z(1, m_c, prod_c[:], gained_b[:, :, QUARTER:HALF], 85)
-        y_max(0, *pairs[1])
+        round_z(1, m_b, prod_b[:, :, 0:QUARTER], gained_b[:, :, 0:QUARTER], 82)
+        round_z(1, m_c, prod_b[:, :, QUARTER:HALF], gained_b[:, :, QUARTER:HALF], 85)
+        quantize_z(1, m_b)
         quantize_z(1, m_c)
-        y_max(0, *pairs[2])
         y_pass(0, m_b, mixed)
         for sums in quarter_banks:
-            y_pass(1, m_b, sums)
-        for sums in quarter_banks:
             y_pass(0, m_c, sums)
+        for sums in quarter_banks:
+            y_pass(1, m_b, sums)
+        y_max(0, *pairs[1])
+        y_max(0, *pairs[2])
         y_copy(m_b, fours[0][0], 23)
         y_copy(m_b, mixed, 25)
         y_max(m_b, *fours[0])

from contextlib import ExitStack

import concourse.mybir as mybir

K, T, S, M, H, N = 1536, 4096, 1024, 512, 1024, 768
FLOPS = 2 * K * H * S + 2 * 2 * H * N * M

F32 = mybir.dt.float32
BF16 = mybir.dt.bfloat16
I32 = mybir.dt.int32
U32 = mybir.dt.uint32
U16 = mybir.dt.uint16
U8 = mybir.dt.uint8
FP8X4 = mybir.dt.float8_e4m3fn_x4
FP4X4 = mybir.dt.float4_e2m1fn_x4
ACT = mybir.ActivationFunctionType
MULT = mybir.AluOpType.mult
MAX = mybir.AluOpType.max

P = 128
PACK = 4
PASS = P * PACK
K_PASSES = K // PASS
R_PASSES = H // PASS
QUADRANTS = 4
LIST_GROUP = 16
BANK = 512
LINE = 4
HALF = M // 2
QUARTER = M // 4
N_TILES = N // P
RIM, BODY, BASE = 0, 1, 2
OX, RD = 0, 1


def tile_list_sherd_vessel_joining_kernel(
    tc, tab_words, tab_scales, offs, pos1, pos2, pos3, w1, gain, wox_words, wox_scales, wrd, out
):
    nc = tc.nc
    with ExitStack() as ctx:
        keep = ctx.enter_context(tc.tile_pool(name="keep", bufs=1))
        ring = ctx.enter_context(tc.tile_pool(name="ring", bufs=4))
        shared = ctx.enter_context(tc.tile_pool(name="shared", bufs=1))
        psum = ctx.enter_context(tc.psum_pool(name="psum", bufs=8))

        def kept(shape, dtype, name):
            return keep.tile(shape, dtype, name=name, align_bytes=64)

        def placed(shape, dtype, name, kib):
            return shared.tile(shape, dtype, name=name, align_bytes=64, offset=int(1024 * kib))

        def load_rows(src, name, a, col0, width, kib):
            raw = placed([P, PACK, width], F32, name, kib)
            rows = src[a * PASS : (a + 1) * PASS, col0 : col0 + width]
            nc.sync.dma_start(raw[:], rows.rearrange("(p j) c -> p j c", j=PACK))
            return raw

        def load_list(entries, name):
            tile = keep.tile(list(entries.shape), U16, name=name)
            nc.sync.dma_start(tile[:], entries)
            return tile

        def load_words(a, c0, c1):
            src = tab_words[a].rearrange("p t i -> p (t i)").bitcast(I32)
            nc.sync.dma_start(tab_w[a][:, c0:c1].bitcast(I32), src[:, c0:c1])

        tab_sc = [placed([P, T], U8, "tab_sc%d" % a, (96, 100, 46)[a]) for a in range(K_PASSES)]
        v_sc = kept([P, K_PASSES, S], U8, "v_sc")
        for tile in tab_sc:
            nc.vector.memset(tile[:].bitcast(I32), 0)
        nc.vector.memset(v_sc[:].rearrange("p a j -> p (a j)").bitcast(I32), 0)

        raw = {}
        tab_w = [placed([P, T], U32, "tab_w%d" % a, (16, 0, 32)[a]) for a in range(K_PASSES)]
        load_words(0, 0, T // 2)
        offs_t = load_list(offs, "offs_t")
        for a in range(K_PASSES):
            nc.sync.dma_start(tab_sc[a][0:P:8, :].bitcast(I32), tab_scales[a].bitcast(I32))
        load_words(0, T // 2, T)
        raw[(0, 0)] = load_rows(w1, "w1_00", 0, 0, PASS, 88)
        pos_t = [load_list(pos, "pos_t%d" % which) for which, pos in enumerate((pos1, pos2))]
        load_words(1, 0, T)
        pos_t.append(load_list(pos3, "pos_t2"))
        raw[(0, 1)] = load_rows(w1, "w1_01", 1, 0, PASS, 114)

        picked_sc = placed([P, K_PASSES, S], U8, "picked_sc", 78)
        for a in range(K_PASSES):
            nc.vector.tensor_copy(picked_sc[:, a, :], tab_sc[a][:].indirect(offs_t[:]))
        for r in range(4):
            nc.sync.dma_start(
                v_sc[r:P:32].rearrange("p a j -> p (a j)").bitcast(I32),
                picked_sc[8 * r : P : 32].rearrange("p a j -> p (a j)").bitcast(I32),
            )
        load_words(2, 0, T)
        raw[(0, 2)] = load_rows(w1, "w1_02", 2, 0, PASS, 48)

        warm = keep.tile([P, 2], F32, name="warm")
        nc.vector.memset(warm[:], 0.0)
        nc.scalar.activation(warm[:, 1:2], warm[:, 0:1], ACT.Abs_reciprocal_sqrt, bias=1.0)

        v_w = [placed([P, S], U32, "v_w0", 96)] + [kept([P, S], U32, "v_w%d" % a) for a in range(1, K_PASSES)]

        def quantize(name, rounded, kib=None):
            width = rounded.shape[1] // PACK
            scales = kept([P, width], U8, name + "_scales")
            codes = kept([P, width], U32, name + "_codes") if kib is None else placed([P, width], U32, name + "_codes", kib)
            nc.vector.quantize_mx(out=codes[:].bitcast(FP8X4), scales=scales[:], in_=rounded)
            return codes, scales

        def blocks(pair):
            codes, scales = pair
            return [(codes[:, c : c + P], scales[:, c : c + P]) for c in range(0, codes.shape[1], P)]

        def round_w1(b, a, u, dst, copy):
            src = raw[(b, a)][:].rearrange("p j (m t) -> p m j t", t=PACK)
            copy(dst.rearrange("p (s m j) -> p m j s", s=2, j=PACK), src[:, :, :, 2 * u : 2 * u + 2])

        w1_q, h_ps, h_sb = {}, {}, {}

        def quantize_w1(name, rounded, a, tiles):
            for g, block in zip(tiles, blocks(quantize(name, rounded))):
                w1_q[(g, a)] = block

        def h_pass(g, bank, a):
            if a == 0:
                h_ps[(g, bank)] = psum.tile([P, BANK], F32, name="bank", tag="bank")
            codes, scales = w1_q[(g, a)]
            cols = slice(bank * BANK, (bank + 1) * BANK)
            nc.tensor.matmul_mx(
                out=h_ps[(g, bank)][:],
                lhsT=codes.bitcast(FP8X4),
                lhsT_scale=scales,
                rhs=v_w[a][:, cols].bitcast(FP8X4),
                rhs_scale=v_sc[:, a, cols],
                start=(a == 0),
                stop=(a == K_PASSES - 1),
            )

        def h_out(g, bank):
            if bank == 0:
                h_sb[g] = kept([P, S], F32, "h%d" % g)
            nc.scalar.copy(h_sb[g][:, bank * BANK : (bank + 1) * BANK], h_ps[(g, bank)][:])

        def picked(g, which, m0, width):
            return h_sb[g][:].indirect(pos_t[which][:, m0 // LIST_GROUP : (m0 + width) // LIST_GROUP])

        def scalar_pick(dst, src):
            nc.scalar.activation(dst, src, ACT.Copy)

        for a in range(K_PASSES):
            nc.vector.tensor_copy(v_w[a][:], tab_w[a][:].indirect(offs_t[:]))
            for u in range(2):
                rounded = ring.tile([P, 2 * PACK * P], BF16, name="narrow", tag="narrow", align_bytes=64)
                round_w1(0, a, u, rounded[:], nc.vector.tensor_copy if (a, u) == (K_PASSES - 1, 0) else nc.scalar.copy)
                if (a, u) == (K_PASSES - 1, 0):
                    for s in range(2):
                        quantize_w1("w1_last%d" % s, rounded[:, s * PASS : (s + 1) * PASS], a, [s])
                else:
                    quantize_w1("w1_0%d%d" % (a, u), rounded[:], a, [2 * u, 2 * u + 1])
            for g in range(PACK):
                for bank in range(S // BANK):
                    h_pass(g, bank, a)
        for a in range(K_PASSES):
            raw[(1, a)] = load_rows(w1, "w1_1%d" % a, a, PASS, PASS, (16, 24, 88)[a])
        wrd_raw = [load_rows(wrd, "wrd_raw%d" % b, b, 0, N, 32 * b) for b in range(R_PASSES)]
        wox_w = placed([P, R_PASSES, 2 * N], U8, "wox_w", 12)
        wox_sc = placed([P, R_PASSES, N], U8, "wox_sc", 120)
        nc.vector.memset(wox_sc[:].rearrange("p b n -> p (b n)").bitcast(I32), 0)
        gain_t = placed([P, R_PASSES * PACK], F32, "gain_t", 121.5)
        nc.sync.dma_start(
            gain_t[:].rearrange("p (b t) -> p b t", t=PACK), gain.rearrange("(b p t) -> p b t", b=R_PASSES, t=PACK)
        )
        nc.sync.dma_start(wox_w[:].bitcast(I32), wox_words.rearrange("b p c -> p b c").bitcast(I32))
        for q in range(QUADRANTS):
            nc.sync.dma_start(
                wox_sc[32 * q : 32 * q + 4, :, :].bitcast(I32),
                wox_scales[:, 4 * q : 4 * q + 4, :].rearrange("b r n -> r b n").bitcast(I32),
            )

        late_first = kept([P, PACK * PASS], BF16, "late_first")
        late_rest = placed([P, K_PASSES - 1, PACK * PASS], BF16, "late_rest", 106)

        def round_late(a):
            dst = late_first[:] if a == 0 else late_rest[:, a - 1, :]
            for u in range(2):
                round_w1(1, a, u, dst[:, 2 * u * PASS : 2 * (u + 1) * PASS], nc.vector.tensor_copy)

        wrd_rounded = placed([P, R_PASSES * PACK * N], BF16, "wrd_rounded", 60)
        wrd_q = []

        def round_wrd(b):
            nc.vector.tensor_copy(
                wrd_rounded[:, b * PACK * N : (b + 1) * PACK * N].rearrange("p (c i j) -> p c j i", i=LINE, j=PACK),
                wrd_raw[b][:].rearrange("p j (c i) -> p c j i", i=LINE),
            )

        def quantize_wrd(c0, width, kib=None):
            wrd_q.extend(blocks(quantize("wrd_%d" % c0, wrd_rounded[:, c0 : c0 + width], kib)))

        body, z_rounded, z_q = {}, {}, {}

        def pick_body(g, m0, width, kib=None):
            name = "body%d_%d" % (g, m0)
            body[(g, m0)] = kept([P, width], F32, name) if kib is None else placed([P, width], F32, name, kib)
            scalar_pick(body[(g, m0)][:], picked(g, BODY, m0, width))

        def pick_rim(g, m0, rims, pick=scalar_pick):
            pick(rims[:, g % PACK, :], picked(g, RIM, m0, rims.shape[2]))

        def pick_base(g, m0, products):
            dst = products[:, g % PACK, :]
            nc.vector.tensor_tensor(dst, picked(g, BASE, m0, dst.shape[1]), body[(g, m0)][:], MULT)

        def square(dst, src):
            nc.scalar.activation(dst, src, ACT.Square)

        def inverse_root(dst, src):
            nc.scalar.activation(dst, src, ACT.Abs_reciprocal_sqrt, bias=1.0)

        def gained_square(g, gained, roots):
            root = roots[:, g % PACK, :]
            nc.vector.scalar_tensor_tensor(gained[:, g % PACK, :], root, gain_t[:, g : g + 1], root, MULT, MULT)

        def round_z(b, m0, products, damping, kib):
            z_rounded[(b, m0)] = placed([P, PACK * damping.shape[2]], BF16, "z_rounded%d_%d" % (b, m0), kib)
            nc.vector.tensor_tensor(
                z_rounded[(b, m0)][:].rearrange("p (c i t) -> p c t i", i=LINE, t=PACK),
                products.rearrange("p t (c i) -> p c t i", i=LINE),
                damping.rearrange("p t (c i) -> p c t i", i=LINE),
                MULT,
            )

        def quantize_z(b, m0):
            z_q[(b, m0)] = quantize("z_%d_%d" % (b, m0), z_rounded[(b, m0)][:])

        late_tiles = range(PACK, 2 * PACK)
        roots = placed([P, PACK, M], F32, "roots0", 48)
        prod0 = placed([P, PACK, M], F32, "prod0", 88)
        for a in range(K_PASSES):
            round_late(a)
        h_out(0, 0)
        h_out(0, 1)
        h_out(1, 0)
        h_out(1, 1)
        pick_rim(0, 0, roots, nc.vector.tensor_copy)
        quantize_w1("late_first", late_first[:], 0, late_tiles)
        pick_rim(1, 0, roots, nc.vector.tensor_copy)
        for i, block in enumerate(blocks(quantize("late_rest", late_rest[:].rearrange("p a c -> p (a c)")))):
            w1_q[(PACK + i % PACK, 1 + i // PACK)] = block
        for g in late_tiles:
            for bank in range(S // BANK):
                for a in range(K_PASSES):
                    h_pass(g, bank, a)
        pick_body(0, 0, M)
        h_out(2, 0)
        h_out(2, 1)
        pick_rim(2, 0, roots, nc.vector.tensor_copy)
        pick_body(1, 0, M)
        square(roots[:, 0:2, :], roots[:, 0:2, :])
        h_out(3, 0)
        inverse_root(roots[:, 0:2, :], roots[:, 0:2, :])
        h_out(3, 1)
        pick_body(2, 0, M)
        pick_rim(3, 0, roots)
        h_out(4, 0)
        square(roots[:, 2:PACK, :], roots[:, 2:PACK, :])
        pick_body(3, 0, M)
        inverse_root(roots[:, 2:PACK, :], roots[:, 2:PACK, :])
        pick_base(0, 0, prod0)
        pick_base(1, 0, prod0)
        gained0 = placed([P, PACK, M], F32, "gained0", 106)
        gained_square(0, gained0, roots)
        gained_square(1, gained0, roots)
        pick_base(2, 0, prod0)
        pick_base(3, 0, prod0)
        gained_square(2, gained0, roots)
        gained_square(3, gained0, roots)
        round_wrd(0)
        round_z(0, 0, prod0[:], gained0[:], 56)
        round_wrd(1)
        quantize_z(0, 0)
        quantize_wrd(0, 4096)

        m_b, m_c = HALF, HALF + QUARTER
        rims_a = placed([P, PACK, HALF], F32, "rims_a", 44)
        squares_a = placed([P, PACK, HALF], F32, "squares_a", 102)
        roots_a = placed([P, PACK, HALF], F32, "roots_a", 72)
        prod_a = placed([P, PACK, HALF], F32, "prod_a", 30)
        gained_a = placed([P, PACK, HALF], F32, "gained_a", 36)
        h_out(4, 1)
        for g in late_tiles[:-1]:
            h_out(g + 1, 0)
            h_out(g + 1, 1)
            pick_rim(g, 0, rims_a)
        pick_rim(7, 0, rims_a)
        pick_body(4, 0, HALF)
        pick_body(5, 0, HALF)
        pick_body(6, 0, HALF)
        square(squares_a[:], rims_a[:])
        pick_body(7, 0, HALF, 98)
        inverse_root(roots_a[:], squares_a[:])
        rims_b = placed([P, PACK, HALF], F32, "rims_b", 42)
        for g in late_tiles[:-1]:
            pick_base(g, 0, prod_a)
        for g in late_tiles[0:1]:
            pick_rim(g, HALF, rims_b, nc.vector.tensor_copy)

        y_ps = {}

        def open_bank(m0, width, sums):
            y_ps[(m0, sums)] = psum.tile([P, len(sums), width], F32, name="bank", tag="bank")

        def y_pass(b, m0, sums):
            bank = y_ps[(m0, sums)]
            width = bank.shape[2]
            z_codes, z_scales = z_q[(b, m0 * b)]
            cols = slice(m0 * (1 - b), m0 * (1 - b) + width)
            for u, (style, n) in enumerate(sums):
                if style == OX:
                    codes, scales = wox_w[:, b, 2 * n * P : 2 * (n + 1) * P].bitcast(FP4X4), wox_sc[:, b, n * P : (n + 1) * P]
                else:
                    codes, scales = wrd_q[b * N_TILES + n][0].bitcast(FP8X4), wrd_q[b * N_TILES + n][1]
                nc.tensor.matmul_mx(
                    out=bank[:, u, :],
                    lhsT=codes,
                    lhsT_scale=scales,
                    rhs=z_codes[:, cols].bitcast(FP8X4),
                    rhs_scale=z_scales[:, cols],
                    start=(b == 0 and u == 0),
                    stop=(b == R_PASSES - 1 and u == len(sums) - 1),
                )

        res = {}

        def y_copy(m0, ox_sums, kib):
            bank = y_ps[(m0, ox_sums)]
            count = len([style for style, n in ox_sums if style == OX])
            res[(m0, ox_sums)] = placed([P, count, bank.shape[2]], F32, "res_%d_%d" % (m0, ox_sums[0][1]), kib)
            nc.scalar.copy(res[(m0, ox_sums)][:], bank[:, 0:count, :])

        def y_max(m0, ox_sums, rd_sums):
            tile = res[(m0, ox_sums)]
            count, width = tile.shape[1], tile.shape[2]
            first = len(rd_sums) - count
            n0 = ox_sums[0][1] * P
            nc.vector.tensor_tensor(tile[:], y_ps[(m0, rd_sums)][:, first : first + count, :], tile[:], MAX)
            nc.sync.dma_start(out[n0 : n0 + count * P, m0 : m0 + width].rearrange("(u p) m -> p u m", u=count), tile[:])

        def run_of(style, n0, count):
            return tuple((style, n) for n in range(n0, n0 + count))

        pairs = [(run_of(OX, n0, 2), run_of(RD, n0, 2)) for n0 in range(0, N_TILES, 2)]
        mixed = run_of(OX, 4, 2) + run_of(RD, 4, 2)
        fours = [(run_of(OX, 0, 4), run_of(RD, 0, 4)), (mixed, mixed)]
        quarter_banks = [fours[0][0], fours[0][1], mixed]
        half_banks = [pair[style] for style in (OX, RD) for pair in pairs]
        for sums in half_banks:
            open_bank(0, HALF, sums)
        for m0 in (m_b, m_c):
            for sums in quarter_banks:
                open_bank(m0, QUARTER, sums)
        for sums in half_banks:
            y_pass(0, 0, sums)
        for sums in quarter_banks[0:2]:
            y_pass(0, m_b, sums)

        for g in late_tiles[:-1]:
            gained_square(g, gained_a, roots_a)
        pick_base(7, 0, prod_a)
        gained_square(7, gained_a, roots_a)
        quantize_wrd(4096, 2048, 98.5)

        squares_b = placed([P, PACK, HALF], F32, "squares_b", 88)
        roots_b = placed([P, PACK, HALF], F32, "roots_b", 76)
        prod_b = placed([P, PACK, HALF], F32, "prod_b", 36)
        gained_b = placed([P, PACK, HALF], F32, "gained_b", 30)
        for g in late_tiles[1:]:
            pick_rim(g, HALF, rims_b)
        pick_body(4, HALF, HALF, 102)
        square(squares_b[:], rims_b[:])
        pick_body(5, HALF, HALF, 103)
        inverse_root(roots_b[:], squares_b[:])
        pick_body(6, HALF, HALF, 88)
        pick_body(7, HALF, HALF, 89)
        round_z(1, 0, prod_a[:], gained_a[:], 80)
        quantize_z(1, 0)
        pick_base(4, HALF, prod_b)
        pick_base(5, HALF, prod_b)
        for pair in pairs:
            y_pass(1, 0, pair[OX])
            y_pass(1, 0, pair[RD])
        for i, pair in enumerate(pairs):
            y_copy(0, pair[OX], 17 + 2 * i)
        for g in late_tiles:
            gained_square(g, gained_b, roots_b)
        pick_base(6, HALF, prod_b)
        pick_base(7, HALF, prod_b)
        y_max(0, *pairs[0])
        round_z(1, m_b, prod_b[:, :, 0:QUARTER], gained_b[:, :, 0:QUARTER], 82)
        round_z(1, m_c, prod_b[:, :, QUARTER:HALF], gained_b[:, :, QUARTER:HALF], 85)
        quantize_z(1, m_b)
        quantize_z(1, m_c)
        y_pass(0, m_b, mixed)
        for sums in quarter_banks:
            y_pass(0, m_c, sums)
        for sums in quarter_banks:
            y_pass(1, m_b, sums)
        y_max(0, *pairs[1])
        y_max(0, *pairs[2])
        y_copy(m_b, fours[0][0], 23)
        y_copy(m_b, mixed, 25)
        y_max(m_b, *fours[0])
        y_max(m_b, *fours[1])
        for sums in quarter_banks:
            y_pass(1, m_c, sums)
        y_copy(m_c, fours[0][0], 26)
        y_copy(m_c, mixed, 28)
        y_max(m_c, *fours[0])
        y_max(m_c, *fours[1])
